import numpy as np
import ml_dtypes


def mxq(x, axis, fmt="e4m3"):
    dtype, down = {"e4m3": (ml_dtypes.float8_e4m3fn, 7), "e5m2": (ml_dtypes.float8_e5m2, 14)}[fmt]
    v = np.moveaxis(np.asarray(x, np.float32).astype(ml_dtypes.bfloat16).astype(np.float64), axis, -1)
    blocks = v.reshape(v.shape[:-1] + (-1, 32))
    amax = np.abs(blocks).max(-1, keepdims=True)
    byte = np.maximum(np.where(amax > 0, np.frexp(amax)[1] - 1 + 127, 0) - down, 1)
    scale = np.exp2(byte - 127.0)
    codes = (blocks / scale).astype(np.float32).astype(dtype).astype(np.float64)
    return np.moveaxis((codes * scale).reshape(v.shape), -1, axis)


WIDE = False


def mx_kscale(k, group=512):
    if not WIDE:
        return np.ones(k)
    levels = np.array([10, -10, 5, -5, 0])
    if group != 512:
        return np.exp2(np.random.permutation(np.resize(levels, k // group))).repeat(group)
    if k % 512:
        return np.exp2(np.random.permutation(np.resize(levels, k // 32))).repeat(32)
    a = np.empty((k // 512, 16))
    for p in range(k // 512):
        a[p, :8] = np.random.permutation(np.resize(levels, 8))
        for g in range(8):
            far = levels[np.abs(levels - a[p, g]) >= 10]
            a[p, g + 8] = far[np.random.randint(len(far))]
    return np.exp2(a.ravel()).repeat(32)


def f64(x):
    return np.asarray(x).astype(np.float64)


G, D, M, O, N = 2, 256, 256, 256, 512


def sgn(shape):
    return np.random.uniform(0.5, 2.0, shape) * np.where(np.random.standard_normal(shape) < 0, -1.0, 1.0)


def setup_inputs():
    n = np.random.standard_normal
    s_d = mx_kscale(D, 0)
    s_m = mx_kscale(M, 0)
    return {
        "x": (n((G, D, N)) * s_d[:, None]).astype(np.float32),
        "w1": (n((G, D, M)) / np.sqrt(D) / s_d[:, None]).astype(np.float32),
        "w2": (n((G, D, M)) / np.sqrt(D) / s_d[:, None]).astype(np.float32),
        "fl": (np.random.uniform(0.05, 0.3, (G, M, 1))).astype(np.float32),
        "hs": (sgn((G, M, 1)) * s_m[:, None]).astype(np.float32),
        "wo2": (n((G, M, O)) / np.sqrt(M) / s_m[:, None]).astype(np.float32),
        "ob": (0.5 * n((G, O, 1))).astype(np.float32),
        "osc": (np.random.uniform(0.5, 2.0, (G, O, 1))).astype(np.float32),
    }


def reference(x, w1, w2, fl, hs, wo2, ob, osc):
    w1q = mxq(f64(w1), 1, "e4m3")
    xq = mxq(f64(x), 1, "e4m3")
    z1 = w1q.transpose(0, 2, 1) @ xq
    w2q = mxq(f64(w2), 1, "e4m3")
    z2 = w2q.transpose(0, 2, 1) @ xq
    e1 = np.exp(np.square(z1) * (-1.0))
    e2 = np.exp(np.square(z2) * (-1.0))
    h = e1 / (e1 + e2 + f64(fl)) * z2
    hh = h * f64(hs)
    wo2q = mxq(f64(wo2), 1, "e4m3")
    hhq = mxq(hh, 1, "e4m3")
    y0 = wo2q.transpose(0, 2, 1) @ hhq
    y = np.tanh(y0 + f64(ob)) * f64(osc)
    return y

@@ -1,0 +1,238 @@
+from contextlib import ExitStack
+
+import concourse.mybir as mybir
+
+G, D, M, O, N = 2, 256, 256, 256, 512
+FLOPS = 2 * G * N * (2 * D * M + M * O)
+
+F32 = mybir.dt.float32
+BF16 = mybir.dt.bfloat16
+U32 = mybir.dt.uint32
+U8 = mybir.dt.uint8
+FP8X4 = mybir.dt.float8_e4m3fn_x4
+ACT = mybir.ActivationFunctionType
+ALU = mybir.AluOpType
+
+P = 128
+ROWS = 64
+PACK = 4
+CH = 128
+HALF = 256
+
+
+def tile_rows_fgaussshare_kernel(tc, x, w1, w2, fl, hs, wo2, ob, osc, out):
+    nc = tc.nc
+    with ExitStack() as ctx:
+        sb = ctx.enter_context(tc.tile_pool(name="sb", bufs=1))
+        ps = ctx.enter_context(tc.psum_pool(name="ps", bufs=1))
+        ctx.enter_context(tc.manual_schedule())
+
+        def tl(name, shape, dtype):
+            return sb.tile(shape, dtype, name=name, align_bytes=64)
+
+        def rows(g):
+            return slice(ROWS * g, ROWS * (g + 1))
+
+        bank = [[ps.tile([P, 512], F32, name="bank_%d_%d" % (g, i)) for i in range(4)] for g in range(G)]
+        z2_bank = [[bank[g][h] for h in range(2)] for g in range(G)]
+        z1_bank = [[bank[g][2 + h] for h in range(2)] for g in range(G)]
+
+        w2_raw = tl("w2_raw", [P, PACK, M], F32)
+        w1_raw = tl("w1_raw", [P, PACK, M], F32)
+        wo_raw = tl("wo_raw", [P, PACK, O], F32)
+        x_raw = [tl("x_raw%d" % h, [P, PACK, HALF], F32) for h in range(2)]
+        fl_t = tl("fl_t", [P, G, 2], F32)
+        hs_t = tl("hs_t", [P, G, 2], F32)
+        ob_t = tl("ob_t", [P, G * 2], F32)
+        osc_t = tl("osc_t", [P, G * 2], F32)
+        x_v = x.rearrange("g (p j) n -> (g p) j n", j=PACK)
+        nc.sync.dma_start(out=w2_raw[:], in_=w2.rearrange("g (p j) m -> (g p) j m", j=PACK))
+        nc.scalar.dma_start(out=hs_t[:], in_=hs.rearrange("g (q t) o -> q g (t o)", t=2))
+        nc.scalar.dma_start(out=fl_t[:], in_=fl.rearrange("g (q t) o -> q g (t o)", t=2))
+        for h in range(2):
+            nc.sync.dma_start(out=x_raw[h][:], in_=x_v[:, :, h * HALF:(h + 1) * HALF])
+        nc.sync.dma_start(out=w1_raw[:], in_=w1.rearrange("g (p j) m -> (g p) j m", j=PACK))
+        nc.sync.dma_start(out=wo_raw[:], in_=wo2.rearrange("g (p j) m -> (g p) j m", j=PACK))
+        with nc.allow_non_contiguous_dma(reason="one value a partition"):
+            nc.sync.dma_start(out=ob_t[:], in_=ob.rearrange("g (u q) o -> q (g u o)", q=P))
+            nc.sync.dma_start(out=osc_t[:], in_=osc.rearrange("g (u q) o -> q (g u o)", q=P))
+
+        def mx_tiles(name, width):
+            return (tl(name + "_bf", [P, width * PACK], BF16), tl(name + "_c", [P, width], U32), tl(name + "_s", [P, width], U8))
+
+        def quantize(t, c0, c1):
+            bf, codes, scales = t
+            nc.vector.quantize_mx(out=codes[:, c0:c1].bitcast(FP8X4), scales=scales[:, c0:c1], in_=bf[:, PACK * c0:PACK * c1])
+
+        def interleave(t, raw, c0, c1):
+            nc.vector.tensor_copy(
+                out=t[0][:, PACK * c0:PACK * c1].rearrange("p (c i j) -> p c j i", i=4, j=PACK),
+                in_=raw[:, :, c0:c1].rearrange("p j (c i) -> p c j i", i=4),
+            )
+
+        def interleave_dealt(t, raw):
+            nc.vector.tensor_copy(
+                out=t[0][:].rearrange("p (t c e j) -> p c j e t", t=2, e=2, j=PACK),
+                in_=raw[:].rearrange("p j (c e t) -> p c j e t", e=2, t=2),
+            )
+
+        def mm(dst, g, w, wcols, a, acols):
+            nc.tensor.matmul_mx(
+                out=dst,
+                lhsT=w[1][rows(g), wcols].bitcast(FP8X4),
+                lhsT_scale=w[2][rows(g), wcols],
+                rhs=a[1][rows(g), acols].bitcast(FP8X4),
+                rhs_scale=a[2][rows(g), acols],
+                start=True,
+                stop=True,
+            )
+
+        def layer1(banks, w, h):
+            for g in range(G):
+                for t in range(2):
+                    for e in range(2):
+                        mm(banks[g][h][:, t * HALF + e * CH:t * HALF + (e + 1) * CH], g, w, slice(t * P, (t + 1) * P),
+                           xq[h], slice(e * CH, (e + 1) * CH))
+
+        w1q = mx_tiles("w1", M)
+        w2q = mx_tiles("w2", M)
+        woq = mx_tiles("wo", O)
+        xq = [mx_tiles("x%d" % h, HALF) for h in range(2)]
+
+        sq2 = [[tl("sq2_%d_%d" % (h, g), [P, 2, HALF], F32) for g in range(G)] for h in range(2)]
+        e2 = [[tl("e2_%d_%d" % (h, g), [P, 2, HALF], F32) for g in range(G)] for h in range(2)]
+        lg = [[tl("lg_%d_%d" % (h, g), [P, 2, HALF], F32) for g in range(G)] for h in range(2)]
+        sq1 = [[tl("sq1_%d_%d" % (h, g), [P, HALF, 2], F32) for g in range(G)] for h in range(2)]
+        z1s = [tl("z1s_%d" % g, [P, HALF, 2], F32) for g in range(G)]
+        zh = [[tl("zh_%d_%d" % (h, g), [P, HALF, 2], F32) for g in range(G)] for h in range(2)]
+        zh_t = [tl("zht_%d" % h, [P, 2, HALF * 2], F32) for h in range(2)]
+        v = [[tl("v_%d_%d" % (h, g), [P, HALF, 2], F32) for g in range(G)] for h in range(2)]
+        v_t = [tl("vt_%d" % c, [P, 2, CH * 2], F32) for c in range(4)]
+        sg = [tl("sg_%d" % c, [P, 2, CH * 2], F32) for c in range(4)]
+        hq = [mx_tiles("hq%d" % c, CH) for c in range(4)]
+        hs_safe = tl("hs_safe", [P, G * 2], F32)
+        hs_inv = tl("hs_inv", [P, G * 2], F32)
+
+        def pairs(b):
+            return b[:].rearrange("p (t n) -> p n t", t=2)
+
+        def make_zh(h, g):
+            nc.vector.tensor_tensor(out=zh[h][g][:], in0=pairs(z2_bank[g][h]),
+                                    in1=hs_t[:, g, :].unsqueeze(1).to_broadcast([P, HALF, 2]), op=ALU.mult)
+            nc.sync.dma_start(out=zh_t[h][rows(g), :, :], in_=zh[h][g][:].rearrange("p n t -> p (n t)"))
+
+        def exp2(h, g):
+            nc.scalar.activation(out=e2[h][g][:], in_=sq2[h][g][:], func=ACT.Exp, scale=-1.0)
+
+        interleave_dealt(w2q, w2_raw)
+        quantize(w2q, 0, M)
+        for e in range(2):
+            interleave(xq[0], x_raw[0], e * CH, (e + 1) * CH)
+        for e in range(2):
+            quantize(xq[0], e * CH, (e + 1) * CH)
+        layer1(z2_bank, w2q, 0)
+        for g in range(G):
+            nc.scalar.activation(out=sq2[0][g][:].rearrange("p t n -> p (t n)"), in_=z2_bank[g][0][:], func=ACT.Square)
+        for g in range(G):
+            exp2(0, g)
+
+        hs_flat = hs_t[:].rearrange("p g t -> p (g t)")
+        interleave(xq[1], x_raw[1], 0, HALF)
+        nc.vector.scalar_tensor_tensor(out=hs_safe[:], in0=hs_flat, scalar=0.0, in1=hs_flat, op0=ALU.is_equal, op1=ALU.add)
+        quantize(xq[1], 0, HALF)
+        layer1(z2_bank, w2q, 1)
+        interleave_dealt(w1q, w1_raw)
+        nc.vector.reciprocal(out=hs_inv[:], in_=hs_safe[:])
+        quantize(w1q, 0, M)
+        layer1(z1_bank, w1q, 0)
+        layer1(z1_bank, w1q, 1)
+
+        for g in range(G):
+            make_zh(1, g)
+        for g in range(G):
+            for t in range(2):
+                nc.vector.scalar_tensor_tensor(
+                    out=sq2[1][g][:, t, :], in0=z2_bank[g][1][:, t * HALF:(t + 1) * HALF],
+                    scalar=hs_inv[:, 2 * g + t:2 * g + t + 1], in1=zh[1][g][:, :, t], op0=ALU.mult, op1=ALU.mult)
+        for g in range(G):
+            nc.scalar.activation(out=sq1[0][g][:], in_=pairs(z1_bank[g][0]), func=ACT.Square)
+        for g in range(G):
+            exp2(1, g)
+
+        for g in range(G):
+            make_zh(0, g)
+        for g in range(G):
+            nc.vector.tensor_copy(out=z1s[g][:], in_=pairs(z1_bank[g][1]))
+        for g in range(G):
+            nc.vector.tensor_tensor(out=sq1[1][g][:], in0=pairs(z1_bank[g][1]), in1=z1s[g][:], op=ALU.mult)
+
+        for h in range(2):
+            for g in range(G):
+                for t in range(2):
+                    nc.scalar.activation(out=lg[h][g][:, t, :], in_=e2[h][g][:, t, :], func=ACT.Ln, bias=fl_t[:, g, t:t + 1])
+                nc.vector.tensor_tensor(out=v[h][g][:], in0=sq1[h][g][:], in1=lg[h][g][:].rearrange("p t n -> p n t"), op=ALU.add)
+                for e in range(2):
+                    nc.sync.dma_start(out=v_t[2 * h + e][rows(g), :, :],
+                                      in_=v[h][g][:, e * CH:(e + 1) * CH, :].rearrange("p n t -> p (n t)"))
+
+        interleave(woq, wo_raw, 0, O)
+
+        def sigm(c):
+            nc.scalar.activation(out=sg[c][:].rearrange("p x r -> p (x r)"), in_=v_t[c][:].rearrange("p x r -> p (x r)"),
+                                 func=ACT.Sigmoid, scale=-1.0)
+
+        def hidden(c):
+            h, e = divmod(c, 2)
+            nc.vector.tensor_tensor(
+                out=hq[c][0][:].rearrange("p (n x t) -> p n x t", x=2, t=2),
+                in0=sg[c][:].rearrange("p x (n t) -> p n x t", t=2),
+                in1=zh_t[h][:, :, e * CH * 2:(e + 1) * CH * 2].rearrange("p x (n t) -> p n x t", t=2),
+                op=ALU.mult)
+
+        pieces = [(0, 2, 2), (2, 1, 3), (3, 1, 0)]
+        th = [tl("th_%d" % i, [P, G * 2, k * CH], F32) for i, (c0, k, b) in enumerate(pieces)]
+        res = [tl("res_%d" % i, [P, G * 2, k * CH], F32) for i, (c0, k, b) in enumerate(pieces)]
+        out_v = out.rearrange("g (u q) n -> q (g u) n", q=P)
+
+        def layer2(c):
+            quantize(hq[c], 0, CH)
+            for i, (c0, k, b) in enumerate(pieces):
+                if c0 <= c < c0 + k:
+                    for g in range(G):
+                        for u in range(2):
+                            col = (u * k + c - c0) * CH
+                            mm(bank[g][b][:, col:col + CH], g, woq, slice(u * P, (u + 1) * P), hq[c], slice(0, CH))
+
+        def tanh(i):
+            c0, k, b = pieces[i]
+            for g in range(G):
+                for u in range(2):
+                    gu = 2 * g + u
+                    nc.scalar.activation(out=th[i][:, gu, :], in_=bank[g][b][:, u * k * CH:(u + 1) * k * CH],
+                                         func=ACT.Tanh, bias=ob_t[:, gu:gu + 1])
+
+        def finish(i):
+            c0, k, b = pieces[i]
+            for g in range(G):
+                for u in range(2):
+                    gu = 2 * g + u
+                    nc.vector.tensor_scalar(out=res[i][:, gu, :], in0=th[i][:, gu, :], scalar1=osc_t[:, gu:gu + 1],
+                                            scalar2=None, op0=ALU.mult)
+                nc.sync.dma_start(out=out_v[:, 2 * g:2 * g + 2, c0 * CH:(c0 + k) * CH], in_=res[i][:, 2 * g:2 * g + 2, :])
+
+        warm = tl("warm", [P, 2], F32)
+        nc.scalar.activation(out=warm[:], in_=lg[1][1][:, 1, 0:2], func=ACT.Sigmoid)
+        for c in range(4):
+            sigm(c)
+        quantize(woq, 0, O)
+        hidden(0)
+        hidden(1)
+        layer2(0)
+        layer2(1)
+        hidden(2)
+        hidden(3)
+        layer2(2)
+        layer2(3)
+        for i in range(len(pieces)):
+            tanh(i)
+            finish(i)

@@ -18,6 +18,9 @@ ROWS = 64
 PACK = 4
 CH = 128
 HALF = 256
+QUAD = 32
+MOVE_V = (True, True)
+PIECES = [(0, 1, 2), (1, 1, 3), (2, 1, 0), (3, 1, 1)]
 
 
 def tile_rows_fgaussshare_kernel(tc, x, w1, w2, fl, hs, wo2, ob, osc, out):
@@ -41,21 +44,54 @@ def tile_rows_fgaussshare_kernel(tc, x, w1, w2, fl, hs, wo2, ob, osc, out):
         w1_raw = tl("w1_raw", [P, PACK, M], F32)
         wo_raw = tl("wo_raw", [P, PACK, O], F32)
         x_raw = [tl("x_raw%d" % h, [P, PACK, HALF], F32) for h in range(2)]
-        fl_t = tl("fl_t", [P, G, 2], F32)
-        hs_t = tl("hs_t", [P, G, 2], F32)
-        ob_t = tl("ob_t", [P, G * 2], F32)
-        osc_t = tl("osc_t", [P, G * 2], F32)
         x_v = x.rearrange("g (p j) n -> (g p) j n", j=PACK)
-        nc.sync.dma_start(out=w2_raw[:], in_=w2.rearrange("g (p j) m -> (g p) j m", j=PACK))
-        nc.scalar.dma_start(out=hs_t[:], in_=hs.rearrange("g (q t) o -> q g (t o)", t=2))
-        nc.scalar.dma_start(out=fl_t[:], in_=fl.rearrange("g (q t) o -> q g (t o)", t=2))
-        for h in range(2):
+
+        def load_w(dst, w):
+            nc.sync.dma_start(out=dst[:], in_=w.rearrange("g (p j) m -> (g p) j m", j=PACK))
+
+        def load_x(h):
             nc.sync.dma_start(out=x_raw[h][:], in_=x_v[:, :, h * HALF:(h + 1) * HALF])
-        nc.sync.dma_start(out=w1_raw[:], in_=w1.rearrange("g (p j) m -> (g p) j m", j=PACK))
-        nc.sync.dma_start(out=wo_raw[:], in_=wo2.rearrange("g (p j) m -> (g p) j m", j=PACK))
-        with nc.allow_non_contiguous_dma(reason="one value a partition"):
-            nc.sync.dma_start(out=ob_t[:], in_=ob.rearrange("g (u q) o -> q (g u o)", q=P))
-            nc.sync.dma_start(out=osc_t[:], in_=osc.rearrange("g (u q) o -> q (g u o)", q=P))
+
+        hs_row = tl("hs_row", [P, P], F32)
+        fl_row = tl("fl_row", [P, P], F32)
+        ob_row = tl("ob_row", [P, P], F32)
+        osc_row = tl("osc_row", [P, P], F32)
+        m_rows = tl("m_rows", [P, 2, P], F32)
+        m_cols = tl("m_cols", [P, 8, QUAD], F32)
+        ob_cols = tl("ob_cols", [P, 4, QUAD], F32)
+        osc_cols = tl("osc_cols", [P, 4, QUAD], F32)
+        hs_t = tl("hs_t", [P, G, 2], F32)
+        hs_safe = tl("hs_safe", [P, G * 2], F32)
+        hs_inv = tl("hs_inv", [P, G * 2], F32)
+
+        def load_m_vec(eng, dst, vec):
+            eng.dma_start(out=dst[0:P:QUAD, :].rearrange("q (g r) -> q g r", g=G), in_=vec.rearrange("g (q r) o -> q g (r o)", q=4))
+
+        def load_o_vec(eng, dst, vec):
+            eng.dma_start(out=dst[0:P:QUAD, :].rearrange("q (k c) -> q k c", c=QUAD),
+                          in_=vec.rearrange("g (u q c) o -> q (g u) (c o)", q=4, c=QUAD))
+
+        def pair_m_vecs():
+            for i, row in enumerate((hs_row, fl_row)):
+                nc.scalar.copy(out=m_rows[:, i, :].rearrange("p (g t c) -> p g t c", g=G, t=2),
+                               in_=row[:].rearrange("p (g c t) -> p g t c", g=G, t=2))
+
+        def turn_m_vecs():
+            nc.vector.transpose(out=m_cols[:].rearrange("p k c -> p (k c)"), in_=m_rows[:].rearrange("p i c -> p (i c)"))
+
+        def hs_parts():
+            nc.vector.tensor_copy(out=hs_t[:].rearrange("p g t -> p (g t)"), in_=m_cols[:, 0:4, 0])
+
+        def hs_guard():
+            flat = hs_t[:].rearrange("p g t -> p (g t)")
+            nc.vector.scalar_tensor_tensor(out=hs_safe[:], in0=flat, scalar=0.0, in1=flat, op0=ALU.is_equal, op1=ALU.add)
+
+        def hs_inverse():
+            nc.vector.reciprocal(out=hs_inv[:], in_=hs_safe[:])
+
+        def turn_o_vecs():
+            nc.vector.transpose(out=ob_cols[:].rearrange("p k c -> p (k c)"), in_=ob_row[:])
+            nc.vector.transpose(out=osc_cols[:].rearrange("p k c -> p (k c)"), in_=osc_row[:])
 
         def mx_tiles(name, width):
             return (tl(name + "_bf", [P, width * PACK], BF16), tl(name + "_c", [P, width], U32), tl(name + "_s", [P, width], U8))
@@ -64,17 +100,19 @@ def tile_rows_fgaussshare_kernel(tc, x, w1, w2, fl, hs, wo2, ob, osc, out):
             bf, codes, scales = t
             nc.vector.quantize_mx(out=codes[:, c0:c1].bitcast(FP8X4), scales=scales[:, c0:c1], in_=bf[:, PACK * c0:PACK * c1])
 
-        def interleave(t, raw, c0, c1):
-            nc.vector.tensor_copy(
-                out=t[0][:, PACK * c0:PACK * c1].rearrange("p (c i j) -> p c j i", i=4, j=PACK),
-                in_=raw[:, :, c0:c1].rearrange("p j (c i) -> p c j i", i=4),
-            )
+        def vcopy(out, in_):
+            nc.vector.tensor_copy(out=out, in_=in_)
 
-        def interleave_dealt(t, raw):
-            nc.vector.tensor_copy(
-                out=t[0][:].rearrange("p (t c e j) -> p c j e t", t=2, e=2, j=PACK),
-                in_=raw[:].rearrange("p j (c e t) -> p c j e t", e=2, t=2),
-            )
+        def acopy(out, in_):
+            nc.scalar.copy(out=out, in_=in_)
+
+        def interleave(cp, t, raw, c0, c1):
+            cp(out=t[0][:, PACK * c0:PACK * c1].rearrange("p (c i j) -> p c j i", i=4, j=PACK),
+               in_=raw[:, :, c0:c1].rearrange("p j (c i) -> p c j i", i=4))
+
+        def interleave_dealt(cp, t, raw):
+            cp(out=t[0][:].rearrange("p (t c e j) -> p c j e t", t=2, e=2, j=PACK),
+               in_=raw[:].rearrange("p j (c e t) -> p c j e t", e=2, t=2))
 
         def mm(dst, g, w, wcols, a, acols):
             nc.tensor.matmul_mx(
@@ -89,8 +127,8 @@ def tile_rows_fgaussshare_kernel(tc, x, w1, w2, fl, hs, wo2, ob, osc, out):
 
         def layer1(banks, w, h):
             for g in range(G):
-                for t in range(2):
-                    for e in range(2):
+                for e in range(2):
+                    for t in range(2):
                         mm(banks[g][h][:, t * HALF + e * CH:t * HALF + (e + 1) * CH], g, w, slice(t * P, (t + 1) * P),
                            xq[h], slice(e * CH, (e + 1) * CH))
 
@@ -99,140 +137,223 @@ def tile_rows_fgaussshare_kernel(tc, x, w1, w2, fl, hs, wo2, ob, osc, out):
         woq = mx_tiles("wo", O)
         xq = [mx_tiles("x%d" % h, HALF) for h in range(2)]
 
-        sq2 = [[tl("sq2_%d_%d" % (h, g), [P, 2, HALF], F32) for g in range(G)] for h in range(2)]
-        e2 = [[tl("e2_%d_%d" % (h, g), [P, 2, HALF], F32) for g in range(G)] for h in range(2)]
-        lg = [[tl("lg_%d_%d" % (h, g), [P, 2, HALF], F32) for g in range(G)] for h in range(2)]
-        sq1 = [[tl("sq1_%d_%d" % (h, g), [P, HALF, 2], F32) for g in range(G)] for h in range(2)]
-        z1s = [tl("z1s_%d" % g, [P, HALF, 2], F32) for g in range(G)]
-        zh = [[tl("zh_%d_%d" % (h, g), [P, HALF, 2], F32) for g in range(G)] for h in range(2)]
+        def hg(name):
+            return [[tl("%s_%d_%d" % (name, h, g), [P, 2 * HALF], F32) for g in range(G)] for h in range(2)]
+
+        sq2, e2, lg, sq1, z1s, z2s, zh, v = [hg(s) for s in ("sq2", "e2", "lg", "sq1", "z1s", "z2s", "zh", "v")]
         zh_t = [tl("zht_%d" % h, [P, 2, HALF * 2], F32) for h in range(2)]
-        v = [[tl("v_%d_%d" % (h, g), [P, HALF, 2], F32) for g in range(G)] for h in range(2)]
-        v_t = [tl("vt_%d" % c, [P, 2, CH * 2], F32) for c in range(4)]
-        sg = [tl("sg_%d" % c, [P, 2, CH * 2], F32) for c in range(4)]
+        v_t = [tl("vt_%d" % c, [P, 4 * CH], F32) for c in range(4)]
+        sg = [tl("sg_%d" % c, [P, 4 * CH], F32) for c in range(4)]
+        hb = [tl("hb_%d" % c, [P, G, 2 * CH], BF16) for c in range(4)]
+        hb_t = [tl("hbt_%d" % c, [P, PACK, CH], BF16) for c in range(4)]
         hq = [mx_tiles("hq%d" % c, CH) for c in range(4)]
-        hs_safe = tl("hs_safe", [P, G * 2], F32)
-        hs_inv = tl("hs_inv", [P, G * 2], F32)
 
         def pairs(b):
             return b[:].rearrange("p (t n) -> p n t", t=2)
 
+        def nt(b):
+            return b[:].rearrange("p (n t) -> p n t", t=2)
+
         def make_zh(h, g):
-            nc.vector.tensor_tensor(out=zh[h][g][:], in0=pairs(z2_bank[g][h]),
+            nc.vector.tensor_tensor(out=nt(zh[h][g]), in0=pairs(z2_bank[g][h]),
                                     in1=hs_t[:, g, :].unsqueeze(1).to_broadcast([P, HALF, 2]), op=ALU.mult)
-            nc.sync.dma_start(out=zh_t[h][rows(g), :, :], in_=zh[h][g][:].rearrange("p n t -> p (n t)"))
+
+        def move_zh(eng, h, g):
+            eng.dma_start(out=zh_t[h][rows(g), :, :], in_=zh[h][g][:])
+
+        def sq2_act(h, g):
+            nc.scalar.activation(out=sq2[h][g][:], in_=z2_bank[g][h][:], func=ACT.Square)
+
+        def sq2_zh(h, g):
+            for t in range(2):
+                nc.vector.scalar_tensor_tensor(
+                    out=sq2[h][g][:, t * HALF:(t + 1) * HALF], in0=z2_bank[g][h][:, t * HALF:(t + 1) * HALF],
+                    scalar=hs_inv[:, 2 * g + t:2 * g + t + 1], in1=nt(zh[h][g])[:, :, t], op0=ALU.mult, op1=ALU.mult)
+
+        def z2_copy(h, g):
+            nc.vector.tensor_copy(out=z2s[h][g][:], in_=z2_bank[g][h][:])
+
+        def sq2_dve(h, g):
+            nc.vector.tensor_tensor(out=sq2[h][g][:], in0=z2_bank[g][h][:], in1=z2s[h][g][:], op=ALU.mult)
 
         def exp2(h, g):
             nc.scalar.activation(out=e2[h][g][:], in_=sq2[h][g][:], func=ACT.Exp, scale=-1.0)
 
-        interleave_dealt(w2q, w2_raw)
-        quantize(w2q, 0, M)
-        for e in range(2):
-            interleave(xq[0], x_raw[0], e * CH, (e + 1) * CH)
-        for e in range(2):
-            quantize(xq[0], e * CH, (e + 1) * CH)
-        layer1(z2_bank, w2q, 0)
-        for g in range(G):
-            nc.scalar.activation(out=sq2[0][g][:].rearrange("p t n -> p (t n)"), in_=z2_bank[g][0][:], func=ACT.Square)
-        for g in range(G):
-            exp2(0, g)
+        def z1_view(h, g):
+            return pairs(z1_bank[g][h]) if MOVE_V[h] else nt(z1_bank[g][h])
 
-        hs_flat = hs_t[:].rearrange("p g t -> p (g t)")
-        interleave(xq[1], x_raw[1], 0, HALF)
-        nc.vector.scalar_tensor_tensor(out=hs_safe[:], in0=hs_flat, scalar=0.0, in1=hs_flat, op0=ALU.is_equal, op1=ALU.add)
-        quantize(xq[1], 0, HALF)
-        layer1(z2_bank, w2q, 1)
-        interleave_dealt(w1q, w1_raw)
-        nc.vector.reciprocal(out=hs_inv[:], in_=hs_safe[:])
-        quantize(w1q, 0, M)
-        layer1(z1_bank, w1q, 0)
-        layer1(z1_bank, w1q, 1)
+        def sq1_act(h, g):
+            nc.scalar.activation(out=nt(sq1[h][g]), in_=z1_view(h, g), func=ACT.Square)
 
-        for g in range(G):
-            make_zh(1, g)
-        for g in range(G):
+        def z1_copy(h, g):
+            nc.vector.tensor_copy(out=nt(z1s[h][g]), in_=z1_view(h, g))
+
+        def sq1_dve(h, g):
+            nc.vector.tensor_tensor(out=nt(sq1[h][g]), in0=z1_view(h, g), in1=nt(z1s[h][g]), op=ALU.mult)
+
+        def ln(h, g):
             for t in range(2):
-                nc.vector.scalar_tensor_tensor(
-                    out=sq2[1][g][:, t, :], in0=z2_bank[g][1][:, t * HALF:(t + 1) * HALF],
-                    scalar=hs_inv[:, 2 * g + t:2 * g + t + 1], in1=zh[1][g][:, :, t], op0=ALU.mult, op1=ALU.mult)
-        for g in range(G):
-            nc.scalar.activation(out=sq1[0][g][:], in_=pairs(z1_bank[g][0]), func=ACT.Square)
-        for g in range(G):
-            exp2(1, g)
+                nc.scalar.activation(out=lg[h][g][:, t * HALF:(t + 1) * HALF], in_=e2[h][g][:, t * HALF:(t + 1) * HALF],
+                                     func=ACT.Ln, bias=m_cols[:, 4 + 2 * g + t, 0:1])
 
-        for g in range(G):
-            make_zh(0, g)
-        for g in range(G):
-            nc.vector.tensor_copy(out=z1s[g][:], in_=pairs(z1_bank[g][1]))
-        for g in range(G):
-            nc.vector.tensor_tensor(out=sq1[1][g][:], in0=pairs(z1_bank[g][1]), in1=z1s[g][:], op=ALU.mult)
+        def add_v(h, g):
+            if MOVE_V[h]:
+                nc.vector.tensor_tensor(out=nt(v[h][g]), in0=nt(sq1[h][g]), in1=pairs(lg[h][g]), op=ALU.add)
+            else:
+                nc.vector.tensor_tensor(out=v[h][g][:], in0=sq1[h][g][:], in1=lg[h][g][:], op=ALU.add)
 
-        for h in range(2):
-            for g in range(G):
-                for t in range(2):
-                    nc.scalar.activation(out=lg[h][g][:, t, :], in_=e2[h][g][:, t, :], func=ACT.Ln, bias=fl_t[:, g, t:t + 1])
-                nc.vector.tensor_tensor(out=v[h][g][:], in0=sq1[h][g][:], in1=lg[h][g][:].rearrange("p t n -> p n t"), op=ALU.add)
-                for e in range(2):
-                    nc.sync.dma_start(out=v_t[2 * h + e][rows(g), :, :],
-                                      in_=v[h][g][:, e * CH:(e + 1) * CH, :].rearrange("p n t -> p (n t)"))
+        def move_v(eng, c, g):
+            h, e = divmod(c, 2)
+            eng.dma_start(out=v_t[c][rows(g), :].rearrange("p (x r) -> p x r", x=2), in_=v[h][g][:, e * 2 * CH:(e + 1) * 2 * CH])
 
-        interleave(woq, wo_raw, 0, O)
+        warm = tl("warm", [P, 2], F32)
+
+        def warm_sigmoid(h, g):
+            nc.scalar.activation(out=warm[:], in_=lg[h][g][:, HALF:HALF + 2], func=ACT.Sigmoid)
 
         def sigm(c):
-            nc.scalar.activation(out=sg[c][:].rearrange("p x r -> p (x r)"), in_=v_t[c][:].rearrange("p x r -> p (x r)"),
-                                 func=ACT.Sigmoid, scale=-1.0)
+            nc.scalar.activation(out=sg[c][:], in_=v_t[c][:], func=ACT.Sigmoid, scale=-1.0)
+
+        def sigm_s(h, g):
+            nc.scalar.activation(out=e2[h][g][:], in_=v[h][g][:], func=ACT.Sigmoid, scale=-1.0)
 
         def hidden(c):
             h, e = divmod(c, 2)
             nc.vector.tensor_tensor(
                 out=hq[c][0][:].rearrange("p (n x t) -> p n x t", x=2, t=2),
-                in0=sg[c][:].rearrange("p x (n t) -> p n x t", t=2),
+                in0=sg[c][:].rearrange("p (x n t) -> p n x t", x=2, t=2),
                 in1=zh_t[h][:, :, e * CH * 2:(e + 1) * CH * 2].rearrange("p x (n t) -> p n x t", t=2),
                 op=ALU.mult)
 
-        pieces = [(0, 2, 2), (2, 1, 3), (3, 1, 0)]
-        th = [tl("th_%d" % i, [P, G * 2, k * CH], F32) for i, (c0, k, b) in enumerate(pieces)]
-        res = [tl("res_%d" % i, [P, G * 2, k * CH], F32) for i, (c0, k, b) in enumerate(pieces)]
+        hbh = [[tl("hbh_%d_%d" % (h, g), [P, 2, 2, CH], BF16) for g in range(G)] for h in range(2)]
+
+        def hidden_s(h, g):
+            for t in range(2):
+                nc.vector.scalar_tensor_tensor(
+                    out=hbh[h][g][:, :, t, :], in0=e2[h][g][:, t * HALF:(t + 1) * HALF].rearrange("p (e n) -> p e n", e=2),
+                    scalar=hs_t[:, g, t:t + 1],
+                    in1=z2_bank[g][h][:, t * HALF:(t + 1) * HALF].rearrange("p (e n) -> p e n", e=2), op0=ALU.mult, op1=ALU.mult)
+
+        def move_h(eng, c, g):
+            h, e = divmod(c, 2)
+            eng.dma_start(out=hb_t[c][rows(g), :, :].rearrange("p (x t) n -> p x (t n)", x=2),
+                          in_=hbh[h][g][:, e, :, :].rearrange("p t n -> p (t n)"))
+
+        def hidden_il(cp, c):
+            interleave(cp, hq[c], hb_t[c], 0, CH)
+
+        th = [tl("th_%d" % i, [P, G * 2, k * CH], F32) for i, (c0, k, b) in enumerate(PIECES)]
+        res = [tl("res_%d" % i, [P, G * 2, k * CH], F32) for i, (c0, k, b) in enumerate(PIECES)]
         out_v = out.rearrange("g (u q) n -> q (g u) n", q=P)
 
         def layer2(c):
             quantize(hq[c], 0, CH)
-            for i, (c0, k, b) in enumerate(pieces):
+            for i, (c0, k, b) in enumerate(PIECES):
                 if c0 <= c < c0 + k:
                     for g in range(G):
                         for u in range(2):
                             col = (u * k + c - c0) * CH
                             mm(bank[g][b][:, col:col + CH], g, woq, slice(u * P, (u + 1) * P), hq[c], slice(0, CH))
 
-        def tanh(i):
-            c0, k, b = pieces[i]
-            for g in range(G):
-                for u in range(2):
-                    gu = 2 * g + u
-                    nc.scalar.activation(out=th[i][:, gu, :], in_=bank[g][b][:, u * k * CH:(u + 1) * k * CH],
-                                         func=ACT.Tanh, bias=ob_t[:, gu:gu + 1])
+        def tanh(i, g):
+            c0, k, b = PIECES[i]
+            for u in range(2):
+                gu = 2 * g + u
+                nc.scalar.activation(out=th[i][:, gu, :], in_=bank[g][b][:, u * k * CH:(u + 1) * k * CH],
+                                     func=ACT.Tanh, bias=ob_cols[:, gu, 0:1])
 
-        def finish(i):
-            c0, k, b = pieces[i]
-            for g in range(G):
-                for u in range(2):
-                    gu = 2 * g + u
-                    nc.vector.tensor_scalar(out=res[i][:, gu, :], in0=th[i][:, gu, :], scalar1=osc_t[:, gu:gu + 1],
-                                            scalar2=None, op0=ALU.mult)
-                nc.sync.dma_start(out=out_v[:, 2 * g:2 * g + 2, c0 * CH:(c0 + k) * CH], in_=res[i][:, 2 * g:2 * g + 2, :])
+        def finish(i, g):
+            c0, k, b = PIECES[i]
+            for u in range(2):
+                gu = 2 * g + u
+                nc.vector.tensor_scalar(out=res[i][:, gu, :], in0=th[i][:, gu, :], scalar1=osc_cols[:, gu, 0:1],
+                                        scalar2=None, op0=ALU.mult)
+            nc.sync.dma_start(out=out_v[:, 2 * g:2 * g + 2, c0 * CH:(c0 + k) * CH], in_=res[i][:, 2 * g:2 * g + 2, :])
 
-        warm = tl("warm", [P, 2], F32)
-        nc.scalar.activation(out=warm[:], in_=lg[1][1][:, 1, 0:2], func=ACT.Sigmoid)
-        for c in range(4):
-            sigm(c)
+        for row in (hs_row, fl_row, ob_row, osc_row):
+            nc.vector.memset(row[:], 0.0)
+        load_w(w2_raw, w2)
+        load_m_vec(nc.sync, hs_row, hs)
+        load_m_vec(nc.sync, fl_row, fl)
+        load_x(0)
+        load_x(1)
+        load_w(w1_raw, w1)
+        load_w(wo_raw, wo2)
+        load_o_vec(nc.sync, ob_row, ob)
+        load_o_vec(nc.sync, osc_row, osc)
+        interleave_dealt(vcopy, w2q, w2_raw)
+        pair_m_vecs()
+        quantize(w2q, 0, M)
+        turn_m_vecs()
+        interleave(vcopy, xq[0], x_raw[0], 0, 160)
+        interleave(acopy, xq[0], x_raw[0], 160, HALF)
+        hs_parts()
+        quantize(xq[0], 0, HALF)
+        hs_guard()
+        layer1(z2_bank, w2q, 0)
+        interleave(vcopy, xq[1], x_raw[1], 0, CH)
+        interleave(vcopy, xq[1], x_raw[1], CH, HALF)
+        quantize(xq[1], 0, CH)
+        quantize(xq[1], CH, HALF)
+        layer1(z2_bank, w2q, 1)
+        for g in range(G):
+            sq2_act(0, g)
+        for g in range(G):
+            exp2(0, g)
+        interleave_dealt(vcopy, w1q, w1_raw)
+        hs_inverse()
+        quantize(w1q, 0, M)
+        layer1(z1_bank, w1q, 0)
+        layer1(z1_bank, w1q, 1)
+        for g in range(G):
+            make_zh(1, g)
+            move_zh(nc.sync, 1, g)
+        for g in range(G):
+            sq2_zh(1, g)
+        for g in range(G):
+            sq1_act(0, g)
+        for g in range(G):
+            exp2(1, g)
+        for g in range(G):
+            make_zh(0, g)
+            move_zh(nc.sync, 0, g)
+        for g in range(G):
+            z1_copy(1, g)
+        for g in range(G):
+            sq1_dve(1, g)
+        ln(0, 0)
+        add_v(0, 0)
+        move_v(nc.sync, 0, 0)
+        move_v(nc.sync, 1, 0)
+        ln(0, 1)
+        add_v(0, 1)
+        ln(1, 0)
+        add_v(1, 0)
+        move_v(nc.sync, 2, 0)
+        ln(1, 1)
+        move_v(nc.scalar, 0, 1)
+        move_v(nc.scalar, 1, 1)
+        add_v(1, 1)
+        move_v(nc.sync, 2, 1)
+        move_v(nc.sync, 3, 0)
+        warm_sigmoid(1, 1)
+        move_v(nc.scalar, 3, 1)
+        interleave(vcopy, woq, wo_raw, 0, O)
+        turn_o_vecs()
+        sigm(0)
+        sigm(1)
         quantize(woq, 0, O)
         hidden(0)
         hidden(1)
         layer2(0)
-        layer2(1)
+        sigm(2)
         hidden(2)
+        layer2(1)
+        sigm(3)
         hidden(3)
         layer2(2)
         layer2(3)
-        for i in range(len(pieces)):
-            tanh(i)
-            finish(i)
+        for i in range(len(PIECES)):
+            for g in range(G):
+                tanh(i, g)
+                finish(i, g)

@@ -19,8 +19,7 @@ PACK = 4
 CH = 128
 HALF = 256
 QUAD = 32
-MOVE_V = (True, True)
-PIECES = [(0, 1, 2), (1, 1, 3), (2, 1, 0), (3, 1, 1)]
+XS = 288
 
 
 def tile_rows_fgaussshare_kernel(tc, x, w1, w2, fl, hs, wo2, ob, osc, out):
@@ -43,14 +42,14 @@ def tile_rows_fgaussshare_kernel(tc, x, w1, w2, fl, hs, wo2, ob, osc, out):
         w2_raw = tl("w2_raw", [P, PACK, M], F32)
         w1_raw = tl("w1_raw", [P, PACK, M], F32)
         wo_raw = tl("wo_raw", [P, PACK, O], F32)
-        x_raw = [tl("x_raw%d" % h, [P, PACK, HALF], F32) for h in range(2)]
+        x_raw = tl("x_raw", [P, PACK, N], F32)
         x_v = x.rearrange("g (p j) n -> (g p) j n", j=PACK)
 
         def load_w(dst, w):
             nc.sync.dma_start(out=dst[:], in_=w.rearrange("g (p j) m -> (g p) j m", j=PACK))
 
-        def load_x(h):
-            nc.sync.dma_start(out=x_raw[h][:], in_=x_v[:, :, h * HALF:(h + 1) * HALF])
+        def load_x():
+            nc.sync.dma_start(out=x_raw[:], in_=x_v)
 
         hs_row = tl("hs_row", [P, P], F32)
         fl_row = tl("fl_row", [P, P], F32)
@@ -73,7 +72,7 @@ def tile_rows_fgaussshare_kernel(tc, x, w1, w2, fl, hs, wo2, ob, osc, out):
 
         def pair_m_vecs():
             for i, row in enumerate((hs_row, fl_row)):
-                nc.scalar.copy(out=m_rows[:, i, :].rearrange("p (g t c) -> p g t c", g=G, t=2),
+                nc.vector.tensor_copy(out=m_rows[:, i, :].rearrange("p (g t c) -> p g t c", g=G, t=2),
                                in_=row[:].rearrange("p (g c t) -> p g t c", g=G, t=2))
 
         def turn_m_vecs():
@@ -114,6 +113,10 @@ def tile_rows_fgaussshare_kernel(tc, x, w1, w2, fl, hs, wo2, ob, osc, out):
             cp(out=t[0][:].rearrange("p (t c e j) -> p c j e t", t=2, e=2, j=PACK),
                in_=raw[:].rearrange("p j (c e t) -> p c j e t", e=2, t=2))
 
+        def interleave_dealt_t(cp, tq, raw, t):
+            cp(out=tq[0][:, t * 512:(t + 1) * 512].rearrange("p (c e j) -> p c j e", e=2, j=PACK),
+               in_=raw[:].rearrange("p j (c e t) -> p c j e t", e=2, t=2)[:, :, :, :, t])
+
         def mm(dst, g, w, wcols, a, acols):
             nc.tensor.matmul_mx(
                 out=dst,
@@ -125,235 +128,227 @@ def tile_rows_fgaussshare_kernel(tc, x, w1, w2, fl, hs, wo2, ob, osc, out):
                 stop=True,
             )
 
-        def layer1(banks, w, h):
-            for g in range(G):
-                for e in range(2):
-                    for t in range(2):
-                        mm(banks[g][h][:, t * HALF + e * CH:t * HALF + (e + 1) * CH], g, w, slice(t * P, (t + 1) * P),
-                           xq[h], slice(e * CH, (e + 1) * CH))
-
         w1q = mx_tiles("w1", M)
         w2q = mx_tiles("w2", M)
         woq = mx_tiles("wo", O)
-        xq = [mx_tiles("x%d" % h, HALF) for h in range(2)]
+        xq = mx_tiles("x", N)
+        hq = mx_tiles("hq", N)
 
-        def hg(name):
-            return [[tl("%s_%d_%d" % (name, h, g), [P, 2 * HALF], F32) for g in range(G)] for h in range(2)]
+        def layer1(banks, w, t):
+            for g in range(G):
+                mm(banks[g][t][:], g, w, slice(t * P, (t + 1) * P), xq, slice(0, N))
 
-        sq2, e2, lg, sq1, z1s, z2s, zh, v = [hg(s) for s in ("sq2", "e2", "lg", "sq1", "z1s", "z2s", "zh", "v")]
-        zh_t = [tl("zht_%d" % h, [P, 2, HALF * 2], F32) for h in range(2)]
-        v_t = [tl("vt_%d" % c, [P, 4 * CH], F32) for c in range(4)]
-        sg = [tl("sg_%d" % c, [P, 4 * CH], F32) for c in range(4)]
-        hb = [tl("hb_%d" % c, [P, G, 2 * CH], BF16) for c in range(4)]
-        hb_t = [tl("hbt_%d" % c, [P, PACK, CH], BF16) for c in range(4)]
-        hq = [mx_tiles("hq%d" % c, CH) for c in range(4)]
+        def gt(name):
+            return [[tl("%s_%d_%d" % (name, g, t), [P, N], F32) for t in range(2)] for g in range(G)]
 
-        def pairs(b):
-            return b[:].rearrange("p (t n) -> p n t", t=2)
+        sq2, e2, lg, sq1, z1s, zh = [gt(s) for s in ("sq2", "e2", "lg", "sq1", "z1s", "zh")]
+        zh_t = tl("zht", [P, 2, 2, N], F32)
+        zi = [tl("zi_%d" % h, [P, HALF, PACK], F32) for h in range(2)]
+        sq1g = [tl("sq1g_%d" % g, [P, 2, N], F32) for g in range(G)]
+        lgg = [[tl("lgg_%d_%d" % (h, g), [P, 2, HALF], F32) for g in range(G)] for h in range(2)]
+        v = [[tl("v_%d_%d" % (h, g), [P, 2, 2, CH], F32) for g in range(G)] for h in range(2)]
+        v_t = [tl("vt_%d" % c, [P, PACK, CH], F32) for c in range(4)]
+        sg = [tl("sgi_%d" % c, [P, CH, PACK], F32) for c in range(4)]
 
-        def nt(b):
-            return b[:].rearrange("p (n t) -> p n t", t=2)
+        def make_zh(g, t):
+            nc.vector.tensor_scalar(out=zh[g][t][:], in0=z2_bank[g][t][:], scalar1=hs_t[:, g, t:t + 1], scalar2=None, op0=ALU.mult)
 
-        def make_zh(h, g):
-            nc.vector.tensor_tensor(out=nt(zh[h][g]), in0=pairs(z2_bank[g][h]),
-                                    in1=hs_t[:, g, :].unsqueeze(1).to_broadcast([P, HALF, 2]), op=ALU.mult)
+        def move_zh(eng, g, t):
+            eng.dma_start(out=zh_t[rows(g), :, t, :], in_=zh[g][t][:])
 
-        def move_zh(eng, h, g):
-            eng.dma_start(out=zh_t[h][rows(g), :, :], in_=zh[h][g][:])
+        def pack_zh(h):
+            nc.vector.tensor_copy(out=zi[h][:], in_=zh_t[:].rearrange("p x t n -> p n (x t)")[:, h * HALF:(h + 1) * HALF, :])
 
-        def sq2_act(h, g):
-            nc.scalar.activation(out=sq2[h][g][:], in_=z2_bank[g][h][:], func=ACT.Square)
+        def sq2_act(g, t):
+            nc.scalar.activation(out=sq2[g][t][:], in_=z2_bank[g][t][:], func=ACT.Square)
 
-        def sq2_zh(h, g):
-            for t in range(2):
-                nc.vector.scalar_tensor_tensor(
-                    out=sq2[h][g][:, t * HALF:(t + 1) * HALF], in0=z2_bank[g][h][:, t * HALF:(t + 1) * HALF],
-                    scalar=hs_inv[:, 2 * g + t:2 * g + t + 1], in1=nt(zh[h][g])[:, :, t], op0=ALU.mult, op1=ALU.mult)
+        def sq2_zh(g, t):
+            nc.vector.scalar_tensor_tensor(out=sq2[g][t][:], in0=z2_bank[g][t][:], scalar=hs_inv[:, 2 * g + t:2 * g + t + 1],
+                                           in1=zh[g][t][:], op0=ALU.mult, op1=ALU.mult)
 
-        def z2_copy(h, g):
-            nc.vector.tensor_copy(out=z2s[h][g][:], in_=z2_bank[g][h][:])
+        def exp2(g, t):
+            nc.scalar.activation(out=e2[g][t][:], in_=sq2[g][t][:], func=ACT.Exp, scale=-1.0)
 
-        def sq2_dve(h, g):
-            nc.vector.tensor_tensor(out=sq2[h][g][:], in0=z2_bank[g][h][:], in1=z2s[h][g][:], op=ALU.mult)
+        def sq1_act(g, t):
+            nc.scalar.activation(out=sq1g[g][:, t, :], in_=z1_bank[g][t][:], func=ACT.Square)
 
-        def exp2(h, g):
-            nc.scalar.activation(out=e2[h][g][:], in_=sq2[h][g][:], func=ACT.Exp, scale=-1.0)
+        def z1_copy(g, t):
+            nc.vector.tensor_copy(out=z1s[g][t][:], in_=z1_bank[g][t][:])
 
-        def z1_view(h, g):
-            return pairs(z1_bank[g][h]) if MOVE_V[h] else nt(z1_bank[g][h])
-
-        def sq1_act(h, g):
-            nc.scalar.activation(out=nt(sq1[h][g]), in_=z1_view(h, g), func=ACT.Square)
-
-        def z1_copy(h, g):
-            nc.vector.tensor_copy(out=nt(z1s[h][g]), in_=z1_view(h, g))
-
-        def sq1_dve(h, g):
-            nc.vector.tensor_tensor(out=nt(sq1[h][g]), in0=z1_view(h, g), in1=nt(z1s[h][g]), op=ALU.mult)
+        def sq1_dve(g, t):
+            nc.vector.tensor_tensor(out=sq1g[g][:, t, :], in0=z1_bank[g][t][:], in1=z1s[g][t][:], op=ALU.mult)
 
         def ln(h, g):
             for t in range(2):
-                nc.scalar.activation(out=lg[h][g][:, t * HALF:(t + 1) * HALF], in_=e2[h][g][:, t * HALF:(t + 1) * HALF],
+                nc.scalar.activation(out=lgg[h][g][:, t, :], in_=e2[g][t][:, h * HALF:(h + 1) * HALF],
                                      func=ACT.Ln, bias=m_cols[:, 4 + 2 * g + t, 0:1])
 
         def add_v(h, g):
-            if MOVE_V[h]:
-                nc.vector.tensor_tensor(out=nt(v[h][g]), in0=nt(sq1[h][g]), in1=pairs(lg[h][g]), op=ALU.add)
-            else:
-                nc.vector.tensor_tensor(out=v[h][g][:], in0=sq1[h][g][:], in1=lg[h][g][:], op=ALU.add)
+            nc.vector.tensor_tensor(out=v[h][g][:],
+                                    in0=sq1g[g][:, :, h * HALF:(h + 1) * HALF].rearrange("p t (e n) -> p e t n", e=2),
+                                    in1=lgg[h][g][:].rearrange("p t (e n) -> p e t n", e=2), op=ALU.add)
 
         def move_v(eng, c, g):
             h, e = divmod(c, 2)
-            eng.dma_start(out=v_t[c][rows(g), :].rearrange("p (x r) -> p x r", x=2), in_=v[h][g][:, e * 2 * CH:(e + 1) * 2 * CH])
+            eng.dma_start(out=v_t[c][rows(g), :, :].rearrange("p (x t) n -> p x (t n)", x=2),
+                          in_=v[h][g][:, e, :, :].rearrange("p t n -> p (t n)"))
 
         warm = tl("warm", [P, 2], F32)
 
         def warm_sigmoid(h, g):
-            nc.scalar.activation(out=warm[:], in_=lg[h][g][:, HALF:HALF + 2], func=ACT.Sigmoid)
+            nc.scalar.activation(out=warm[:], in_=lgg[h][g][:, 1, 0:2], func=ACT.Sigmoid)
 
-        def sigm(c):
-            nc.scalar.activation(out=sg[c][:], in_=v_t[c][:], func=ACT.Sigmoid, scale=-1.0)
+        def sigm(c, a=0, b=CH):
+            nc.scalar.activation(out=sg[c][:, a:b, :], in_=v_t[c][:].rearrange("p j n -> p n j")[:, a:b, :], func=ACT.Sigmoid, scale=-1.0)
+
+        def hidden(c, a=0, b=CH):
+            h, e = divmod(c, 2)
+            nc.vector.tensor_tensor(out=hq[0][:, PACK * (c * CH + a):PACK * (c * CH + b)],
+                                    in0=sg[c][:, a:b, :].rearrange("p n j -> p (n j)"),
+                                    in1=zi[h][:, e * CH + a:e * CH + b, :].rearrange("p n j -> p (n j)"), op=ALU.mult)
+
+        def quant_h(c, a=0, b=CH):
+            quantize(hq, c * CH + a, c * CH + b)
+
+        z2s = gt("z2s")
+        vg = [tl("vg_%d" % g, [P, 2, N], F32) for g in range(G)]
+        share = [[tl("share_%d_%d" % (h, g), [P, 2, HALF], F32) for g in range(G)] for h in range(2)]
+        hb = [[tl("hb_%d_%d" % (h, g), [P, 2, 2, CH], BF16) for g in range(G)] for h in range(2)]
+        hb_t = [tl("hbt_%d" % c, [P, PACK, CH], BF16) for c in range(4)]
+
+        def z2_copy(g, t):
+            nc.vector.tensor_copy(out=z2s[g][t][:], in_=z2_bank[g][t][:])
+
+        def sq2_dve(g, t):
+            nc.vector.tensor_tensor(out=sq2[g][t][:], in0=z2_bank[g][t][:], in1=z2s[g][t][:], op=ALU.mult)
+
+        def ln_s(g, t):
+            nc.scalar.activation(out=lg[g][t][:], in_=e2[g][t][:], func=ACT.Ln, bias=m_cols[:, 4 + 2 * g + t, 0:1])
+
+        def add_s(g, t):
+            nc.vector.tensor_tensor(out=vg[g][:, t, :], in0=sq1g[g][:, t, :], in1=lg[g][t][:], op=ALU.add)
 
         def sigm_s(h, g):
-            nc.scalar.activation(out=e2[h][g][:], in_=v[h][g][:], func=ACT.Sigmoid, scale=-1.0)
-
-        def hidden(c):
-            h, e = divmod(c, 2)
-            nc.vector.tensor_tensor(
-                out=hq[c][0][:].rearrange("p (n x t) -> p n x t", x=2, t=2),
-                in0=sg[c][:].rearrange("p (x n t) -> p n x t", x=2, t=2),
-                in1=zh_t[h][:, :, e * CH * 2:(e + 1) * CH * 2].rearrange("p x (n t) -> p n x t", t=2),
-                op=ALU.mult)
-
-        hbh = [[tl("hbh_%d_%d" % (h, g), [P, 2, 2, CH], BF16) for g in range(G)] for h in range(2)]
+            nc.scalar.activation(out=share[h][g][:], in_=vg[g][:, :, h * HALF:(h + 1) * HALF], func=ACT.Sigmoid, scale=-1.0)
 
         def hidden_s(h, g):
             for t in range(2):
                 nc.vector.scalar_tensor_tensor(
-                    out=hbh[h][g][:, :, t, :], in0=e2[h][g][:, t * HALF:(t + 1) * HALF].rearrange("p (e n) -> p e n", e=2),
-                    scalar=hs_t[:, g, t:t + 1],
-                    in1=z2_bank[g][h][:, t * HALF:(t + 1) * HALF].rearrange("p (e n) -> p e n", e=2), op0=ALU.mult, op1=ALU.mult)
+                    out=hb[h][g][:, :, t, :], in0=share[h][g][:, t, :].rearrange("p (e n) -> p e n", e=2),
+                    scalar=m_cols[:, 2 * g + t, 0:1],
+                    in1=z2_bank[g][t][:, h * HALF:(h + 1) * HALF].rearrange("p (e n) -> p e n", e=2), op0=ALU.mult, op1=ALU.mult)
+
+        def sigm_c(c, g):
+            h, e = divmod(c, 2)
+            nc.scalar.activation(out=share[h][g][:, :, e * CH:(e + 1) * CH], in_=vg[g][:, :, c * CH:(c + 1) * CH], func=ACT.Sigmoid, scale=-1.0)
+
+        def hidden_c(c, g):
+            h, e = divmod(c, 2)
+            for t in range(2):
+                nc.vector.scalar_tensor_tensor(
+                    out=hb[h][g][:, e, t, :], in0=share[h][g][:, t, e * CH:(e + 1) * CH], scalar=m_cols[:, 2 * g + t, 0:1],
+                    in1=z2_bank[g][t][:, c * CH:(c + 1) * CH], op0=ALU.mult, op1=ALU.mult)
 
         def move_h(eng, c, g):
             h, e = divmod(c, 2)
             eng.dma_start(out=hb_t[c][rows(g), :, :].rearrange("p (x t) n -> p x (t n)", x=2),
-                          in_=hbh[h][g][:, e, :, :].rearrange("p t n -> p (t n)"))
+                          in_=hb[h][g][:, e, :, :].rearrange("p t n -> p (t n)"))
 
-        def hidden_il(cp, c):
-            interleave(cp, hq[c], hb_t[c], 0, CH)
+        def pack_h(cp, c, a=0, b=CH):
+            cp(out=hq[0][:, PACK * (c * CH + a):PACK * (c * CH + b)].rearrange("p (c i j) -> p c j i", i=4, j=PACK),
+               in_=hb_t[c][:, :, a:b].rearrange("p j (c i) -> p c j i", i=4))
 
-        th = [tl("th_%d" % i, [P, G * 2, k * CH], F32) for i, (c0, k, b) in enumerate(PIECES)]
-        res = [tl("res_%d" % i, [P, G * 2, k * CH], F32) for i, (c0, k, b) in enumerate(PIECES)]
-        out_v = out.rearrange("g (u q) n -> q (g u) n", q=P)
+        th = gt("th")
+        res = gt("res")
 
-        def layer2(c):
-            quantize(hq[c], 0, CH)
-            for i, (c0, k, b) in enumerate(PIECES):
-                if c0 <= c < c0 + k:
-                    for g in range(G):
-                        for u in range(2):
-                            col = (u * k + c - c0) * CH
-                            mm(bank[g][b][:, col:col + CH], g, woq, slice(u * P, (u + 1) * P), hq[c], slice(0, CH))
-
-        def tanh(i, g):
-            c0, k, b = PIECES[i]
+        def layer2():
             for u in range(2):
-                gu = 2 * g + u
-                nc.scalar.activation(out=th[i][:, gu, :], in_=bank[g][b][:, u * k * CH:(u + 1) * k * CH],
-                                     func=ACT.Tanh, bias=ob_cols[:, gu, 0:1])
+                for g in range(G):
+                    mm(z1_bank[g][u][:], g, woq, slice(u * P, (u + 1) * P), hq, slice(0, N))
 
-        def finish(i, g):
-            c0, k, b = PIECES[i]
-            for u in range(2):
-                gu = 2 * g + u
-                nc.vector.tensor_scalar(out=res[i][:, gu, :], in0=th[i][:, gu, :], scalar1=osc_cols[:, gu, 0:1],
-                                        scalar2=None, op0=ALU.mult)
-            nc.sync.dma_start(out=out_v[:, 2 * g:2 * g + 2, c0 * CH:(c0 + k) * CH], in_=res[i][:, 2 * g:2 * g + 2, :])
+        def finish(g, u, a, b):
+            gu = 2 * g + u
+            nc.scalar.activation(out=th[g][u][:, a:b], in_=z1_bank[g][u][:, a:b], func=ACT.Tanh, bias=ob_cols[:, gu, 0:1])
+            nc.vector.tensor_scalar(out=res[g][u][:, a:b], in0=th[g][u][:, a:b], scalar1=osc_cols[:, gu, 0:1],
+                                    scalar2=None, op0=ALU.mult)
+            nc.sync.dma_start(out=out[g, u * P:(u + 1) * P, a:b], in_=res[g][u][:, a:b])
 
         for row in (hs_row, fl_row, ob_row, osc_row):
             nc.vector.memset(row[:], 0.0)
-        load_w(w2_raw, w2)
+        load_x()
         load_m_vec(nc.sync, hs_row, hs)
         load_m_vec(nc.sync, fl_row, fl)
-        load_x(0)
-        load_x(1)
-        load_w(w1_raw, w1)
-        load_w(wo_raw, wo2)
         load_o_vec(nc.sync, ob_row, ob)
         load_o_vec(nc.sync, osc_row, osc)
-        interleave_dealt(vcopy, w2q, w2_raw)
-        pair_m_vecs()
-        quantize(w2q, 0, M)
-        turn_m_vecs()
-        interleave(vcopy, xq[0], x_raw[0], 0, 160)
-        interleave(acopy, xq[0], x_raw[0], 160, HALF)
-        hs_parts()
-        quantize(xq[0], 0, HALF)
-        hs_guard()
+        load_w(w2_raw, w2)
+        load_w(w1_raw, w1)
+        load_w(wo_raw, wo2)
+        interleave(acopy, xq, x_raw, XS, N)
+        interleave(vcopy, xq, x_raw, 0, 256)
+        interleave(vcopy, xq, x_raw, 256, XS)
+        quantize(xq, 0, 256)
+        interleave_dealt_t(acopy, w2q, w2_raw, 1)
+        interleave_dealt_t(vcopy, w2q, w2_raw, 0)
+        quantize(xq, 256, N)
+        quantize(w2q, 0, P)
         layer1(z2_bank, w2q, 0)
-        interleave(vcopy, xq[1], x_raw[1], 0, CH)
-        interleave(vcopy, xq[1], x_raw[1], CH, HALF)
-        quantize(xq[1], 0, CH)
-        quantize(xq[1], CH, HALF)
+        quantize(w2q, P, M)
         layer1(z2_bank, w2q, 1)
-        for g in range(G):
-            sq2_act(0, g)
-        for g in range(G):
-            exp2(0, g)
-        interleave_dealt(vcopy, w1q, w1_raw)
-        hs_inverse()
-        quantize(w1q, 0, M)
+        interleave_dealt_t(acopy, w1q, w1_raw, 1)
+        interleave_dealt_t(vcopy, w1q, w1_raw, 0)
+        pair_m_vecs()
+        quantize(w1q, 0, P)
         layer1(z1_bank, w1q, 0)
+        quantize(w1q, P, M)
         layer1(z1_bank, w1q, 1)
-        for g in range(G):
-            make_zh(1, g)
-            move_zh(nc.sync, 1, g)
-        for g in range(G):
-            sq2_zh(1, g)
-        for g in range(G):
-            sq1_act(0, g)
-        for g in range(G):
-            exp2(1, g)
-        for g in range(G):
-            make_zh(0, g)
-            move_zh(nc.sync, 0, g)
-        for g in range(G):
-            z1_copy(1, g)
-        for g in range(G):
-            sq1_dve(1, g)
-        ln(0, 0)
-        add_v(0, 0)
-        move_v(nc.sync, 0, 0)
-        move_v(nc.sync, 1, 0)
-        ln(0, 1)
-        add_v(0, 1)
-        ln(1, 0)
-        add_v(1, 0)
-        move_v(nc.sync, 2, 0)
-        ln(1, 1)
-        move_v(nc.scalar, 0, 1)
-        move_v(nc.scalar, 1, 1)
-        add_v(1, 1)
-        move_v(nc.sync, 2, 1)
-        move_v(nc.sync, 3, 0)
-        warm_sigmoid(1, 1)
-        move_v(nc.scalar, 3, 1)
         interleave(vcopy, woq, wo_raw, 0, O)
-        turn_o_vecs()
-        sigm(0)
-        sigm(1)
+        turn_m_vecs()
+        for g in range(G):
+            sq2_act(g, 0)
+        z2_copy(1, 1)
         quantize(woq, 0, O)
-        hidden(0)
-        hidden(1)
-        layer2(0)
-        sigm(2)
-        hidden(2)
-        layer2(1)
-        sigm(3)
-        hidden(3)
-        layer2(2)
-        layer2(3)
-        for i in range(len(PIECES)):
+        sq2_dve(1, 1)
+        for g in range(G):
+            exp2(g, 0)
+        sq2_act(0, 1)
+        exp2(1, 1)
+        exp2(0, 1)
+        rest = [(0, 0), (1, 0), (0, 1), (1, 1)]
+        z1_copy(*rest[0])
+        for i in range(len(rest)):
+            if i + 1 < len(rest):
+                z1_copy(*rest[i + 1])
+            sq1_dve(*rest[i])
+        for g in range(G):
+            for t in range(2):
+                ln_s(g, t)
+                add_s(g, t)
+        turn_o_vecs()
+        for g in range(G):
+            sigm_s(0, g)
+            hidden_s(0, g)
+            move_h(nc.sync, 0, g)
+            move_h(nc.sync, 1, g)
+        sigm_s(1, 0)
+        hidden_s(1, 0)
+        move_h(nc.sync, 2, 0)
+        move_h(nc.sync, 3, 0)
+        for c in (2, 3):
+            sigm_c(c, 1)
+        for c in (2, 3):
+            hidden_c(c, 1)
+            move_h(nc.scalar, c, 1)
+        pack_h(acopy, 0)
+        pack_h(vcopy, 1)
+        quant_h(0)
+        quant_h(1)
+        pack_h(vcopy, 2)
+        pack_h(acopy, 3, 80, CH)
+        pack_h(vcopy, 3, 0, 80)
+        quant_h(2)
+        quant_h(3)
+        layer2()
+        for u in range(2):
             for g in range(G):
-                tanh(i, g)
-                finish(i, g)
+                for h in range(2):
+                    finish(g, u, h * HALF, (h + 1) * HALF)

@@ -16,339 +16,226 @@ ALU = mybir.AluOpType
 P = 128
 ROWS = 64
 PACK = 4
-CH = 128
-HALF = 256
 QUAD = 32
-XS = 288
+CHUNK = 128
+CHUNKS = N // CHUNK
+HALF = N // 2
+X_SPLIT = 288
 
 
 def tile_rows_fgaussshare_kernel(tc, x, w1, w2, fl, hs, wo2, ob, osc, out):
     nc = tc.nc
     with ExitStack() as ctx:
-        sb = ctx.enter_context(tc.tile_pool(name="sb", bufs=1))
-        ps = ctx.enter_context(tc.psum_pool(name="ps", bufs=1))
+        sbuf = ctx.enter_context(tc.tile_pool(name="sbuf", bufs=1))
+        psum = ctx.enter_context(tc.psum_pool(name="psum", bufs=1))
         ctx.enter_context(tc.manual_schedule())
 
-        def tl(name, shape, dtype):
-            return sb.tile(shape, dtype, name=name, align_bytes=64)
+        def alloc(name, shape, dtype):
+            return sbuf.tile(shape, dtype, name=name, align_bytes=64)
+
+        def tiles_gt(name, shape, dtype):
+            return [[alloc("%s_%d_%d" % (name, g, t), shape, dtype) for t in range(2)] for g in range(G)]
 
         def rows(g):
             return slice(ROWS * g, ROWS * (g + 1))
 
-        bank = [[ps.tile([P, 512], F32, name="bank_%d_%d" % (g, i)) for i in range(4)] for g in range(G)]
-        z2_bank = [[bank[g][h] for h in range(2)] for g in range(G)]
-        z1_bank = [[bank[g][2 + h] for h in range(2)] for g in range(G)]
+        def cols(c):
+            return slice(CHUNK * c, CHUNK * (c + 1))
 
-        w2_raw = tl("w2_raw", [P, PACK, M], F32)
-        w1_raw = tl("w1_raw", [P, PACK, M], F32)
-        wo_raw = tl("wo_raw", [P, PACK, O], F32)
-        x_raw = tl("x_raw", [P, PACK, N], F32)
-        x_v = x.rearrange("g (p j) n -> (g p) j n", j=PACK)
-
-        def load_w(dst, w):
-            nc.sync.dma_start(out=dst[:], in_=w.rearrange("g (p j) m -> (g p) j m", j=PACK))
-
-        def load_x():
-            nc.sync.dma_start(out=x_raw[:], in_=x_v)
-
-        hs_row = tl("hs_row", [P, P], F32)
-        fl_row = tl("fl_row", [P, P], F32)
-        ob_row = tl("ob_row", [P, P], F32)
-        osc_row = tl("osc_row", [P, P], F32)
-        m_rows = tl("m_rows", [P, 2, P], F32)
-        m_cols = tl("m_cols", [P, 8, QUAD], F32)
-        ob_cols = tl("ob_cols", [P, 4, QUAD], F32)
-        osc_cols = tl("osc_cols", [P, 4, QUAD], F32)
-        hs_t = tl("hs_t", [P, G, 2], F32)
-        hs_safe = tl("hs_safe", [P, G * 2], F32)
-        hs_inv = tl("hs_inv", [P, G * 2], F32)
-
-        def load_m_vec(eng, dst, vec):
-            eng.dma_start(out=dst[0:P:QUAD, :].rearrange("q (g r) -> q g r", g=G), in_=vec.rearrange("g (q r) o -> q g (r o)", q=4))
-
-        def load_o_vec(eng, dst, vec):
-            eng.dma_start(out=dst[0:P:QUAD, :].rearrange("q (k c) -> q k c", c=QUAD),
-                          in_=vec.rearrange("g (u q c) o -> q (g u) (c o)", q=4, c=QUAD))
-
-        def pair_m_vecs():
-            for i, row in enumerate((hs_row, fl_row)):
-                nc.vector.tensor_copy(out=m_rows[:, i, :].rearrange("p (g t c) -> p g t c", g=G, t=2),
-                               in_=row[:].rearrange("p (g c t) -> p g t c", g=G, t=2))
-
-        def turn_m_vecs():
-            nc.vector.transpose(out=m_cols[:].rearrange("p k c -> p (k c)"), in_=m_rows[:].rearrange("p i c -> p (i c)"))
-
-        def hs_parts():
-            nc.vector.tensor_copy(out=hs_t[:].rearrange("p g t -> p (g t)"), in_=m_cols[:, 0:4, 0])
-
-        def hs_guard():
-            flat = hs_t[:].rearrange("p g t -> p (g t)")
-            nc.vector.scalar_tensor_tensor(out=hs_safe[:], in0=flat, scalar=0.0, in1=flat, op0=ALU.is_equal, op1=ALU.add)
-
-        def hs_inverse():
-            nc.vector.reciprocal(out=hs_inv[:], in_=hs_safe[:])
-
-        def turn_o_vecs():
-            nc.vector.transpose(out=ob_cols[:].rearrange("p k c -> p (k c)"), in_=ob_row[:])
-            nc.vector.transpose(out=osc_cols[:].rearrange("p k c -> p (k c)"), in_=osc_row[:])
-
-        def mx_tiles(name, width):
-            return (tl(name + "_bf", [P, width * PACK], BF16), tl(name + "_c", [P, width], U32), tl(name + "_s", [P, width], U8))
-
-        def quantize(t, c0, c1):
-            bf, codes, scales = t
-            nc.vector.quantize_mx(out=codes[:, c0:c1].bitcast(FP8X4), scales=scales[:, c0:c1], in_=bf[:, PACK * c0:PACK * c1])
-
-        def vcopy(out, in_):
+        def on_vector(out, in_):
             nc.vector.tensor_copy(out=out, in_=in_)
 
-        def acopy(out, in_):
+        def on_scalar(out, in_):
             nc.scalar.copy(out=out, in_=in_)
 
-        def interleave(cp, t, raw, c0, c1):
-            cp(out=t[0][:, PACK * c0:PACK * c1].rearrange("p (c i j) -> p c j i", i=4, j=PACK),
-               in_=raw[:, :, c0:c1].rearrange("p j (c i) -> p c j i", i=4))
+        z2_bank = [[psum.tile([P, N], F32, name="z2_%d_%d" % (g, t)) for t in range(2)] for g in range(G)]
+        z1_bank = [[psum.tile([P, N], F32, name="z1_%d_%d" % (g, t)) for t in range(2)] for g in range(G)]
+        y_bank = z1_bank
 
-        def interleave_dealt(cp, t, raw):
-            cp(out=t[0][:].rearrange("p (t c e j) -> p c j e t", t=2, e=2, j=PACK),
-               in_=raw[:].rearrange("p j (c e t) -> p c j e t", e=2, t=2))
+        def mx_operand(name, width):
+            return (alloc(name + "_bf", [P, width * PACK], BF16), alloc(name + "_codes", [P, width], U32),
+                    alloc(name + "_scales", [P, width], U8))
 
-        def interleave_dealt_t(cp, tq, raw, t):
-            cp(out=tq[0][:, t * 512:(t + 1) * 512].rearrange("p (c e j) -> p c j e", e=2, j=PACK),
-               in_=raw[:].rearrange("p j (c e t) -> p c j e t", e=2, t=2)[:, :, :, :, t])
+        def interleave(copy, values, raw, part, c0, c1):
+            copy(out=values[part, PACK * c0:PACK * c1].rearrange("p (c i j) -> p c j i", i=4, j=PACK),
+                 in_=raw.rearrange("p j (c i) -> p c j i", i=4))
 
-        def mm(dst, g, w, wcols, a, acols):
-            nc.tensor.matmul_mx(
-                out=dst,
-                lhsT=w[1][rows(g), wcols].bitcast(FP8X4),
-                lhsT_scale=w[2][rows(g), wcols],
-                rhs=a[1][rows(g), acols].bitcast(FP8X4),
-                rhs_scale=a[2][rows(g), acols],
-                start=True,
-                stop=True,
-            )
+        def interleave_parity(copy, values, raw, t):
+            copy(out=values[:, PACK * P * t:PACK * P * (t + 1)].rearrange("p (c e j) -> p c j e", e=2, j=PACK),
+                 in_=raw[:].rearrange("p j (c e t) -> p c j e t", e=2, t=2)[:, :, :, :, t])
 
-        w1q = mx_tiles("w1", M)
-        w2q = mx_tiles("w2", M)
-        woq = mx_tiles("wo", O)
-        xq = mx_tiles("x", N)
-        hq = mx_tiles("hq", N)
+        def quantize(values, codes, scales, part, c0, c1):
+            nc.vector.quantize_mx(out=codes[part, c0:c1].bitcast(FP8X4), scales=scales[part, c0:c1],
+                                  in_=values[part, PACK * c0:PACK * c1])
 
-        def layer1(banks, w, t):
+        def matmul(bank, g, weights, t, codes, scales):
+            wcols = slice(P * t, P * (t + 1))
+            nc.tensor.matmul_mx(out=bank[:], lhsT=weights[1][rows(g), wcols].bitcast(FP8X4),
+                                lhsT_scale=weights[2][rows(g), wcols], rhs=codes[rows(g), :].bitcast(FP8X4),
+                                rhs_scale=scales[rows(g), :], start=True, stop=True)
+
+        everywhere = slice(0, P)
+        x_raw = alloc("x_raw", [P, PACK, N], F32)
+        w1_raw = alloc("w1_raw", [P, PACK, M], F32)
+        w2_raw = alloc("w2_raw", [P, PACK, M], F32)
+        wo_raw = alloc("wo_raw", [P, PACK, O], F32)
+        xq = mx_operand("x", N)
+        w1q = mx_operand("w1", M)
+        w2q = mx_operand("w2", M)
+        woq = mx_operand("wo", O)
+
+        def load_operand(dst, src):
+            nc.sync.dma_start(out=dst[:], in_=src.rearrange("g (p j) c -> (g p) j c", j=PACK))
+
+        def first_layer(banks, weights, t):
+            quantize(*weights, everywhere, P * t, P * (t + 1))
             for g in range(G):
-                mm(banks[g][t][:], g, w, slice(t * P, (t + 1) * P), xq, slice(0, N))
+                matmul(banks[g][t], g, weights, t, xq[1], xq[2])
 
-        def gt(name):
-            return [[tl("%s_%d_%d" % (name, g, t), [P, N], F32) for t in range(2)] for g in range(G)]
+        hs_row, fl_row, ob_row, osc_row = [alloc(s + "_row", [P, P], F32) for s in ("hs", "fl", "ob", "osc")]
+        feature_rows = alloc("feature_rows", [P, 2, P], F32)
+        feature_cols = alloc("feature_cols", [P, 2, G, 2, QUAD], F32)
+        ob_cols = alloc("ob_cols", [P, G, 2, QUAD], F32)
+        osc_cols = alloc("osc_cols", [P, G, 2, QUAD], F32)
 
-        sq2, e2, lg, sq1, z1s, zh = [gt(s) for s in ("sq2", "e2", "lg", "sq1", "z1s", "zh")]
-        zh_t = tl("zht", [P, 2, 2, N], F32)
-        zi = [tl("zi_%d" % h, [P, HALF, PACK], F32) for h in range(2)]
-        sq1g = [tl("sq1g_%d" % g, [P, 2, N], F32) for g in range(G)]
-        lgg = [[tl("lgg_%d_%d" % (h, g), [P, 2, HALF], F32) for g in range(G)] for h in range(2)]
-        v = [[tl("v_%d_%d" % (h, g), [P, 2, 2, CH], F32) for g in range(G)] for h in range(2)]
-        v_t = [tl("vt_%d" % c, [P, PACK, CH], F32) for c in range(4)]
-        sg = [tl("sgi_%d" % c, [P, CH, PACK], F32) for c in range(4)]
+        def load_feature_vector(dst, vec):
+            nc.sync.dma_start(out=dst[0:P:QUAD, :].rearrange("r (g c) -> r g c", g=G),
+                              in_=vec.rearrange("g (r c) o -> r g (c o)", r=P // QUAD))
 
-        def make_zh(g, t):
-            nc.vector.tensor_scalar(out=zh[g][t][:], in0=z2_bank[g][t][:], scalar1=hs_t[:, g, t:t + 1], scalar2=None, op0=ALU.mult)
+        def load_output_vector(dst, vec):
+            nc.sync.dma_start(out=dst[0:P:QUAD, :].rearrange("r (k c) -> r k c", c=QUAD),
+                              in_=vec.rearrange("g (u r c) o -> r (g u) (c o)", r=P // QUAD, c=QUAD))
 
-        def move_zh(eng, g, t):
-            eng.dma_start(out=zh_t[rows(g), :, t, :], in_=zh[g][t][:])
+        def split_feature_vectors_by_parity():
+            for i, row in enumerate((hs_row, fl_row)):
+                on_vector(out=feature_rows[:, i, :].rearrange("p (g t c) -> p g t c", g=G, t=2),
+                          in_=row[:].rearrange("p (g c t) -> p g t c", g=G, t=2))
 
-        def pack_zh(h):
-            nc.vector.tensor_copy(out=zi[h][:], in_=zh_t[:].rearrange("p x t n -> p n (x t)")[:, h * HALF:(h + 1) * HALF, :])
+        def turn_feature_vectors():
+            nc.vector.transpose(out=feature_cols[:].rearrange("p i g t c -> p (i g t c)"),
+                                in_=feature_rows[:].rearrange("p i c -> p (i c)"))
 
-        def sq2_act(g, t):
+        def turn_output_vectors():
+            for turned, row in ((ob_cols, ob_row), (osc_cols, osc_row)):
+                nc.vector.transpose(out=turned[:].rearrange("p g u c -> p (g u c)"), in_=row[:])
+
+        z1_copy, z2_copy, sq1, sq2, e2, log_rest = [
+            tiles_gt(s, [P, N], F32) for s in ("z1_copy", "z2_copy", "sq1", "sq2", "e2", "log_rest")]
+        exponent = [alloc("exponent_%d" % g, [P, 2, N], F32) for g in range(G)]
+        share = [[alloc("share_%d_%d" % (g, c), [P, 2, CHUNK], F32) for c in range(CHUNKS)] for g in range(G)]
+        hh = [[alloc("hh_%d_%d" % (g, c), [P, 2, CHUNK], BF16) for c in range(CHUNKS)] for g in range(G)]
+
+        def square_on_scalar(g, t):
             nc.scalar.activation(out=sq2[g][t][:], in_=z2_bank[g][t][:], func=ACT.Square)
 
-        def sq2_zh(g, t):
-            nc.vector.scalar_tensor_tensor(out=sq2[g][t][:], in0=z2_bank[g][t][:], scalar=hs_inv[:, 2 * g + t:2 * g + t + 1],
-                                           in1=zh[g][t][:], op0=ALU.mult, op1=ALU.mult)
+        def copy_out(copies, banks, g, t):
+            on_vector(out=copies[g][t][:], in_=banks[g][t][:])
 
-        def exp2(g, t):
+        def square_on_vector(squares, copies, banks, g, t):
+            nc.vector.tensor_tensor(out=squares[g][t][:], in0=banks[g][t][:], in1=copies[g][t][:], op=ALU.mult)
+
+        def second_bell(g, t):
             nc.scalar.activation(out=e2[g][t][:], in_=sq2[g][t][:], func=ACT.Exp, scale=-1.0)
 
-        def sq1_act(g, t):
-            nc.scalar.activation(out=sq1g[g][:, t, :], in_=z1_bank[g][t][:], func=ACT.Square)
+        def make_exponent(g, t):
+            nc.scalar.activation(out=log_rest[g][t][:], in_=e2[g][t][:], func=ACT.Ln, bias=feature_cols[:, 1, g, t, 0:1])
+            nc.vector.tensor_tensor(out=exponent[g][:, t, :], in0=sq1[g][t][:], in1=log_rest[g][t][:], op=ALU.add)
 
-        def z1_copy(g, t):
-            nc.vector.tensor_copy(out=z1s[g][t][:], in_=z1_bank[g][t][:])
+        hh_moved = [alloc("hh_moved_%d" % c, [P, PACK, CHUNK], BF16) for c in range(CHUNKS)]
 
-        def sq1_dve(g, t):
-            nc.vector.tensor_tensor(out=sq1g[g][:, t, :], in0=z1_bank[g][t][:], in1=z1s[g][t][:], op=ALU.mult)
-
-        def ln(h, g):
+        def make_hidden(g, c):
+            nc.scalar.activation(out=share[g][c][:], in_=exponent[g][:, :, cols(c)], func=ACT.Sigmoid, scale=-1.0)
             for t in range(2):
-                nc.scalar.activation(out=lgg[h][g][:, t, :], in_=e2[g][t][:, h * HALF:(h + 1) * HALF],
-                                     func=ACT.Ln, bias=m_cols[:, 4 + 2 * g + t, 0:1])
+                nc.vector.scalar_tensor_tensor(out=hh[g][c][:, t, :], in0=share[g][c][:, t, :],
+                                               scalar=feature_cols[:, 0, g, t, 0:1], in1=z2_bank[g][t][:, cols(c)],
+                                               op0=ALU.mult, op1=ALU.mult)
+            nc.sync.dma_start(out=hh_moved[c][rows(g), :, :].rearrange("p (s t) n -> p s (t n)", s=2),
+                              in_=hh[g][c][:].rearrange("q t n -> q (t n)"))
 
-        def add_v(h, g):
-            nc.vector.tensor_tensor(out=v[h][g][:],
-                                    in0=sq1g[g][:, :, h * HALF:(h + 1) * HALF].rearrange("p t (e n) -> p e t n", e=2),
-                                    in1=lgg[h][g][:].rearrange("p t (e n) -> p e t n", e=2), op=ALU.add)
+        hh_packed = alloc("hh_packed", [P, N * PACK], BF16)
+        hh_codes = [alloc("hh_codes_%d" % g, [P, N], U32) for g in range(G)]
+        hh_scales = [alloc("hh_scales_%d" % g, [P, N], U8) for g in range(G)]
+        tanh_y = tiles_gt("tanh_y", [P, N], F32)
+        result = tiles_gt("result", [P, N], F32)
 
-        def move_v(eng, c, g):
-            h, e = divmod(c, 2)
-            eng.dma_start(out=v_t[c][rows(g), :, :].rearrange("p (x t) n -> p x (t n)", x=2),
-                          in_=v[h][g][:, e, :, :].rearrange("p t n -> p (t n)"))
+        def pack_hidden(copy, g, c):
+            interleave(copy, hh_packed, hh_moved[c][rows(g), :, :], rows(g), CHUNK * c, CHUNK * (c + 1))
 
-        warm = tl("warm", [P, 2], F32)
+        def quantize_hidden(g, c):
+            quantize(hh_packed, hh_codes[g], hh_scales[g], slice(0, ROWS * (g + 1)), CHUNK * c, CHUNK * (c + 1))
 
-        def warm_sigmoid(h, g):
-            nc.scalar.activation(out=warm[:], in_=lgg[h][g][:, 1, 0:2], func=ACT.Sigmoid)
-
-        def sigm(c, a=0, b=CH):
-            nc.scalar.activation(out=sg[c][:, a:b, :], in_=v_t[c][:].rearrange("p j n -> p n j")[:, a:b, :], func=ACT.Sigmoid, scale=-1.0)
-
-        def hidden(c, a=0, b=CH):
-            h, e = divmod(c, 2)
-            nc.vector.tensor_tensor(out=hq[0][:, PACK * (c * CH + a):PACK * (c * CH + b)],
-                                    in0=sg[c][:, a:b, :].rearrange("p n j -> p (n j)"),
-                                    in1=zi[h][:, e * CH + a:e * CH + b, :].rearrange("p n j -> p (n j)"), op=ALU.mult)
-
-        def quant_h(c, a=0, b=CH):
-            quantize(hq, c * CH + a, c * CH + b)
-
-        z2s = gt("z2s")
-        vg = [tl("vg_%d" % g, [P, 2, N], F32) for g in range(G)]
-        share = [[tl("share_%d_%d" % (h, g), [P, 2, HALF], F32) for g in range(G)] for h in range(2)]
-        hb = [[tl("hb_%d_%d" % (h, g), [P, 2, 2, CH], BF16) for g in range(G)] for h in range(2)]
-        hb_t = [tl("hbt_%d" % c, [P, PACK, CH], BF16) for c in range(4)]
-
-        def z2_copy(g, t):
-            nc.vector.tensor_copy(out=z2s[g][t][:], in_=z2_bank[g][t][:])
-
-        def sq2_dve(g, t):
-            nc.vector.tensor_tensor(out=sq2[g][t][:], in0=z2_bank[g][t][:], in1=z2s[g][t][:], op=ALU.mult)
-
-        def ln_s(g, t):
-            nc.scalar.activation(out=lg[g][t][:], in_=e2[g][t][:], func=ACT.Ln, bias=m_cols[:, 4 + 2 * g + t, 0:1])
-
-        def add_s(g, t):
-            nc.vector.tensor_tensor(out=vg[g][:, t, :], in0=sq1g[g][:, t, :], in1=lg[g][t][:], op=ALU.add)
-
-        def sigm_s(h, g):
-            nc.scalar.activation(out=share[h][g][:], in_=vg[g][:, :, h * HALF:(h + 1) * HALF], func=ACT.Sigmoid, scale=-1.0)
-
-        def hidden_s(h, g):
-            for t in range(2):
-                nc.vector.scalar_tensor_tensor(
-                    out=hb[h][g][:, :, t, :], in0=share[h][g][:, t, :].rearrange("p (e n) -> p e n", e=2),
-                    scalar=m_cols[:, 2 * g + t, 0:1],
-                    in1=z2_bank[g][t][:, h * HALF:(h + 1) * HALF].rearrange("p (e n) -> p e n", e=2), op0=ALU.mult, op1=ALU.mult)
-
-        def sigm_c(c, g):
-            h, e = divmod(c, 2)
-            nc.scalar.activation(out=share[h][g][:, :, e * CH:(e + 1) * CH], in_=vg[g][:, :, c * CH:(c + 1) * CH], func=ACT.Sigmoid, scale=-1.0)
-
-        def hidden_c(c, g):
-            h, e = divmod(c, 2)
-            for t in range(2):
-                nc.vector.scalar_tensor_tensor(
-                    out=hb[h][g][:, e, t, :], in0=share[h][g][:, t, e * CH:(e + 1) * CH], scalar=m_cols[:, 2 * g + t, 0:1],
-                    in1=z2_bank[g][t][:, c * CH:(c + 1) * CH], op0=ALU.mult, op1=ALU.mult)
-
-        def move_h(eng, c, g):
-            h, e = divmod(c, 2)
-            eng.dma_start(out=hb_t[c][rows(g), :, :].rearrange("p (x t) n -> p x (t n)", x=2),
-                          in_=hb[h][g][:, e, :, :].rearrange("p t n -> p (t n)"))
-
-        def pack_h(cp, c, a=0, b=CH):
-            cp(out=hq[0][:, PACK * (c * CH + a):PACK * (c * CH + b)].rearrange("p (c i j) -> p c j i", i=4, j=PACK),
-               in_=hb_t[c][:, :, a:b].rearrange("p j (c i) -> p c j i", i=4))
-
-        th = gt("th")
-        res = gt("res")
-
-        def layer2():
-            for u in range(2):
-                for g in range(G):
-                    mm(z1_bank[g][u][:], g, woq, slice(u * P, (u + 1) * P), hq, slice(0, N))
-
-        def finish(g, u, a, b):
-            gu = 2 * g + u
-            nc.scalar.activation(out=th[g][u][:, a:b], in_=z1_bank[g][u][:, a:b], func=ACT.Tanh, bias=ob_cols[:, gu, 0:1])
-            nc.vector.tensor_scalar(out=res[g][u][:, a:b], in0=th[g][u][:, a:b], scalar1=osc_cols[:, gu, 0:1],
-                                    scalar2=None, op0=ALU.mult)
-            nc.sync.dma_start(out=out[g, u * P:(u + 1) * P, a:b], in_=res[g][u][:, a:b])
+        def finish(g, u, h):
+            half = slice(HALF * h, HALF * (h + 1))
+            nc.scalar.activation(out=tanh_y[g][u][:, half], in_=y_bank[g][u][:, half], func=ACT.Tanh,
+                                 bias=ob_cols[:, g, u, 0:1])
+            nc.vector.tensor_scalar(out=result[g][u][:, half], in0=tanh_y[g][u][:, half],
+                                    scalar1=osc_cols[:, g, u, 0:1], scalar2=None, op0=ALU.mult)
+            nc.sync.dma_start(out=out[g, P * u:P * (u + 1), half], in_=result[g][u][:, half])
 
         for row in (hs_row, fl_row, ob_row, osc_row):
             nc.vector.memset(row[:], 0.0)
-        load_x()
-        load_m_vec(nc.sync, hs_row, hs)
-        load_m_vec(nc.sync, fl_row, fl)
-        load_o_vec(nc.sync, ob_row, ob)
-        load_o_vec(nc.sync, osc_row, osc)
-        load_w(w2_raw, w2)
-        load_w(w1_raw, w1)
-        load_w(wo_raw, wo2)
-        interleave(acopy, xq, x_raw, XS, N)
-        interleave(vcopy, xq, x_raw, 0, 256)
-        interleave(vcopy, xq, x_raw, 256, XS)
-        quantize(xq, 0, 256)
-        interleave_dealt_t(acopy, w2q, w2_raw, 1)
-        interleave_dealt_t(vcopy, w2q, w2_raw, 0)
-        quantize(xq, 256, N)
-        quantize(w2q, 0, P)
-        layer1(z2_bank, w2q, 0)
-        quantize(w2q, P, M)
-        layer1(z2_bank, w2q, 1)
-        interleave_dealt_t(acopy, w1q, w1_raw, 1)
-        interleave_dealt_t(vcopy, w1q, w1_raw, 0)
-        pair_m_vecs()
-        quantize(w1q, 0, P)
-        layer1(z1_bank, w1q, 0)
-        quantize(w1q, P, M)
-        layer1(z1_bank, w1q, 1)
-        interleave(vcopy, woq, wo_raw, 0, O)
-        turn_m_vecs()
+        load_operand(x_raw, x)
+        load_feature_vector(hs_row, hs)
+        load_feature_vector(fl_row, fl)
+        load_output_vector(ob_row, ob)
+        load_output_vector(osc_row, osc)
+        load_operand(w2_raw, w2)
+        load_operand(w1_raw, w1)
+        load_operand(wo_raw, wo2)
+
+        interleave(on_scalar, xq[0], x_raw[:, :, X_SPLIT:N], everywhere, X_SPLIT, N)
+        interleave(on_vector, xq[0], x_raw[:, :, 0:HALF], everywhere, 0, HALF)
+        interleave(on_vector, xq[0], x_raw[:, :, HALF:X_SPLIT], everywhere, HALF, X_SPLIT)
+        quantize(*xq, everywhere, 0, HALF)
+        interleave_parity(on_scalar, w2q[0], w2_raw, 1)
+        interleave_parity(on_vector, w2q[0], w2_raw, 0)
+        quantize(*xq, everywhere, HALF, N)
+        for t in range(2):
+            first_layer(z2_bank, w2q, t)
+        interleave_parity(on_scalar, w1q[0], w1_raw, 1)
+        interleave_parity(on_vector, w1q[0], w1_raw, 0)
+        split_feature_vectors_by_parity()
+        for t in range(2):
+            first_layer(z1_bank, w1q, t)
+
+        square_on_scalar(0, 0)
+        copy_out(z2_copy, z2_bank, 1, 0)
+        turn_output_vectors()
+        square_on_vector(sq2, z2_copy, z2_bank, 1, 0)
+        second_bell(0, 0)
+        square_on_scalar(0, 1)
+        copy_out(z2_copy, z2_bank, 1, 1)
+        turn_feature_vectors()
+        square_on_vector(sq2, z2_copy, z2_bank, 1, 1)
+        second_bell(1, 0)
+        second_bell(0, 1)
+        second_bell(1, 1)
+
+        order = [(g, t) for g in range(G) for t in range(2)]
+        copy_out(z1_copy, z1_bank, *order[0])
+        for i, (g, t) in enumerate(order):
+            if i + 1 < len(order):
+                copy_out(z1_copy, z1_bank, *order[i + 1])
+            square_on_vector(sq1, z1_copy, z1_bank, g, t)
+
+        for g, t in order:
+            make_exponent(g, t)
+
         for g in range(G):
-            sq2_act(g, 0)
-        z2_copy(1, 1)
-        quantize(woq, 0, O)
-        sq2_dve(1, 1)
+            for c in range(CHUNKS):
+                make_hidden(g, c)
+        interleave(on_scalar, woq[0], wo_raw[:], everywhere, 0, O)
         for g in range(G):
-            exp2(g, 0)
-        sq2_act(0, 1)
-        exp2(1, 1)
-        exp2(0, 1)
-        rest = [(0, 0), (1, 0), (0, 1), (1, 1)]
-        z1_copy(*rest[0])
-        for i in range(len(rest)):
-            if i + 1 < len(rest):
-                z1_copy(*rest[i + 1])
-            sq1_dve(*rest[i])
+            for c in range(0, CHUNKS, 2):
+                pack_hidden(on_vector, g, c)
+                pack_hidden(on_scalar, g, c + 1)
+                if (g, c) == (0, 0):
+                    quantize(*woq, everywhere, 0, O)
+            for c in range(CHUNKS):
+                quantize_hidden(g, c)
+            for u in range(2):
+                matmul(y_bank[g][u], g, woq, u, hh_codes[g], hh_scales[g])
         for g in range(G):
-            for t in range(2):
-                ln_s(g, t)
-                add_s(g, t)
-        turn_o_vecs()
-        for g in range(G):
-            sigm_s(0, g)
-            hidden_s(0, g)
-            move_h(nc.sync, 0, g)
-            move_h(nc.sync, 1, g)
-        sigm_s(1, 0)
-        hidden_s(1, 0)
-        move_h(nc.sync, 2, 0)
-        move_h(nc.sync, 3, 0)
-        for c in (2, 3):
-            sigm_c(c, 1)
-        for c in (2, 3):
-            hidden_c(c, 1)
-            move_h(nc.scalar, c, 1)
-        pack_h(acopy, 0)
-        pack_h(vcopy, 1)
-        quant_h(0)
-        quant_h(1)
-        pack_h(vcopy, 2)
-        pack_h(acopy, 3, 80, CH)
-        pack_h(vcopy, 3, 0, 80)
-        quant_h(2)
-        quant_h(3)
-        layer2()
-        for u in range(2):
-            for g in range(G):
+            for u in range(2):
                 for h in range(2):
-                    finish(g, u, h * HALF, (h + 1) * HALF)
+                    finish(g, u, h)

@@ -20,7 +20,7 @@ QUAD = 32
 CHUNK = 128
 CHUNKS = N // CHUNK
 HALF = N // 2
-X_SPLIT = 288
+X_SPLIT = 320
 
 
 def tile_rows_fgaussshare_kernel(tc, x, w1, w2, fl, hs, wo2, ob, osc, out):
@@ -212,19 +212,20 @@ def tile_rows_fgaussshare_kernel(tc, x, w1, w2, fl, hs, wo2, ob, osc, out):
         second_bell(1, 1)
 
         order = [(g, t) for g in range(G) for t in range(2)]
-        copy_out(z1_copy, z1_bank, *order[0])
-        for i, (g, t) in enumerate(order):
-            if i + 1 < len(order):
-                copy_out(z1_copy, z1_bank, *order[i + 1])
-            square_on_vector(sq1, z1_copy, z1_bank, g, t)
+        for g, t in order:
+            copy_out(z1_copy, z1_bank, g, t)
+        for t in range(2):
+            nc.gpsimd.tensor_tensor(out=sq1[0][t][:], in0=z1_copy[0][t][:], in1=z1_copy[0][t][:], op=ALU.mult)
+            square_on_vector(sq1, z1_copy, z1_bank, 1, t)
 
         for g, t in order:
             make_exponent(g, t)
 
+        interleave(on_vector, woq[0], wo_raw[:], everywhere, 0, O)
+
         for g in range(G):
             for c in range(CHUNKS):
                 make_hidden(g, c)
-        interleave(on_scalar, woq[0], wo_raw[:], everywhere, 0, O)
         for g in range(G):
             for c in range(0, CHUNKS, 2):
                 pack_hidden(on_vector, g, c)

from contextlib import ExitStack

import concourse.mybir as mybir

G, D, M, O, N = 2, 256, 256, 256, 512
FLOPS = 2 * G * N * (2 * D * M + M * O)

F32 = mybir.dt.float32
BF16 = mybir.dt.bfloat16
U32 = mybir.dt.uint32
U8 = mybir.dt.uint8
FP8X4 = mybir.dt.float8_e4m3fn_x4
ACT = mybir.ActivationFunctionType
ALU = mybir.AluOpType

P = 128
ROWS = 64
PACK = 4
QUAD = 32
CHUNK = 128
CHUNKS = N // CHUNK
HALF = N // 2
X_SPLIT = 320


def tile_rows_fgaussshare_kernel(tc, x, w1, w2, fl, hs, wo2, ob, osc, out):
    nc = tc.nc
    with ExitStack() as ctx:
        sbuf = ctx.enter_context(tc.tile_pool(name="sbuf", bufs=1))
        psum = ctx.enter_context(tc.psum_pool(name="psum", bufs=1))
        ctx.enter_context(tc.manual_schedule())

        def alloc(name, shape, dtype):
            return sbuf.tile(shape, dtype, name=name, align_bytes=64)

        def tiles_gt(name, shape, dtype):
            return [[alloc("%s_%d_%d" % (name, g, t), shape, dtype) for t in range(2)] for g in range(G)]

        def rows(g):
            return slice(ROWS * g, ROWS * (g + 1))

        def cols(c):
            return slice(CHUNK * c, CHUNK * (c + 1))

        def on_vector(out, in_):
            nc.vector.tensor_copy(out=out, in_=in_)

        def on_scalar(out, in_):
            nc.scalar.copy(out=out, in_=in_)

        z2_bank = [[psum.tile([P, N], F32, name="z2_%d_%d" % (g, t)) for t in range(2)] for g in range(G)]
        z1_bank = [[psum.tile([P, N], F32, name="z1_%d_%d" % (g, t)) for t in range(2)] for g in range(G)]
        y_bank = z1_bank

        def mx_operand(name, width):
            return (alloc(name + "_bf", [P, width * PACK], BF16), alloc(name + "_codes", [P, width], U32),
                    alloc(name + "_scales", [P, width], U8))

        def interleave(copy, values, raw, part, c0, c1):
            copy(out=values[part, PACK * c0:PACK * c1].rearrange("p (c i j) -> p c j i", i=4, j=PACK),
                 in_=raw.rearrange("p j (c i) -> p c j i", i=4))

        def interleave_parity(copy, values, raw, t):
            copy(out=values[:, PACK * P * t:PACK * P * (t + 1)].rearrange("p (c e j) -> p c j e", e=2, j=PACK),
                 in_=raw[:].rearrange("p j (c e t) -> p c j e t", e=2, t=2)[:, :, :, :, t])

        def quantize(values, codes, scales, part, c0, c1):
            nc.vector.quantize_mx(out=codes[part, c0:c1].bitcast(FP8X4), scales=scales[part, c0:c1],
                                  in_=values[part, PACK * c0:PACK * c1])

        def matmul(bank, g, weights, t, codes, scales):
            wcols = slice(P * t, P * (t + 1))
            nc.tensor.matmul_mx(out=bank[:], lhsT=weights[1][rows(g), wcols].bitcast(FP8X4),
                                lhsT_scale=weights[2][rows(g), wcols], rhs=codes[rows(g), :].bitcast(FP8X4),
                                rhs_scale=scales[rows(g), :], start=True, stop=True)

        everywhere = slice(0, P)
        x_raw = alloc("x_raw", [P, PACK, N], F32)
        w1_raw = alloc("w1_raw", [P, PACK, M], F32)
        w2_raw = alloc("w2_raw", [P, PACK, M], F32)
        wo_raw = alloc("wo_raw", [P, PACK, O], F32)
        xq = mx_operand("x", N)
        w1q = mx_operand("w1", M)
        w2q = mx_operand("w2", M)
        woq = mx_operand("wo", O)

        def load_operand(dst, src):
            nc.sync.dma_start(out=dst[:], in_=src.rearrange("g (p j) c -> (g p) j c", j=PACK))

        def first_layer(banks, weights, t):
            quantize(*weights, everywhere, P * t, P * (t + 1))
            for g in range(G):
                matmul(banks[g][t], g, weights, t, xq[1], xq[2])

        hs_row, fl_row, ob_row, osc_row = [alloc(s + "_row", [P, P], F32) for s in ("hs", "fl", "ob", "osc")]
        feature_rows = alloc("feature_rows", [P, 2, P], F32)
        feature_cols = alloc("feature_cols", [P, 2, G, 2, QUAD], F32)
        ob_cols = alloc("ob_cols", [P, G, 2, QUAD], F32)
        osc_cols = alloc("osc_cols", [P, G, 2, QUAD], F32)

        def load_feature_vector(dst, vec):
            nc.sync.dma_start(out=dst[0:P:QUAD, :].rearrange("r (g c) -> r g c", g=G),
                              in_=vec.rearrange("g (r c) o -> r g (c o)", r=P // QUAD))

        def load_output_vector(dst, vec):
            nc.sync.dma_start(out=dst[0:P:QUAD, :].rearrange("r (k c) -> r k c", c=QUAD),
                              in_=vec.rearrange("g (u r c) o -> r (g u) (c o)", r=P // QUAD, c=QUAD))

        def split_feature_vectors_by_parity():
            for i, row in enumerate((hs_row, fl_row)):
                on_vector(out=feature_rows[:, i, :].rearrange("p (g t c) -> p g t c", g=G, t=2),
                          in_=row[:].rearrange("p (g c t) -> p g t c", g=G, t=2))

        def turn_feature_vectors():
            nc.vector.transpose(out=feature_cols[:].rearrange("p i g t c -> p (i g t c)"),
                                in_=feature_rows[:].rearrange("p i c -> p (i c)"))

        def turn_output_vectors():
            for turned, row in ((ob_cols, ob_row), (osc_cols, osc_row)):
                nc.vector.transpose(out=turned[:].rearrange("p g u c -> p (g u c)"), in_=row[:])

        z1_copy, z2_copy, sq1, sq2, e2, log_rest = [
            tiles_gt(s, [P, N], F32) for s in ("z1_copy", "z2_copy", "sq1", "sq2", "e2", "log_rest")]
        exponent = [alloc("exponent_%d" % g, [P, 2, N], F32) for g in range(G)]
        share = [[alloc("share_%d_%d" % (g, c), [P, 2, CHUNK], F32) for c in range(CHUNKS)] for g in range(G)]
        hh = [[alloc("hh_%d_%d" % (g, c), [P, 2, CHUNK], BF16) for c in range(CHUNKS)] for g in range(G)]

        def square_on_scalar(g, t):
            nc.scalar.activation(out=sq2[g][t][:], in_=z2_bank[g][t][:], func=ACT.Square)

        def copy_out(copies, banks, g, t):
            on_vector(out=copies[g][t][:], in_=banks[g][t][:])

        def square_on_vector(squares, copies, banks, g, t):
            nc.vector.tensor_tensor(out=squares[g][t][:], in0=banks[g][t][:], in1=copies[g][t][:], op=ALU.mult)

        def second_bell(g, t):
            nc.scalar.activation(out=e2[g][t][:], in_=sq2[g][t][:], func=ACT.Exp, scale=-1.0)

        def make_exponent(g, t):
            nc.scalar.activation(out=log_rest[g][t][:], in_=e2[g][t][:], func=ACT.Ln, bias=feature_cols[:, 1, g, t, 0:1])
            nc.vector.tensor_tensor(out=exponent[g][:, t, :], in0=sq1[g][t][:], in1=log_rest[g][t][:], op=ALU.add)

        hh_moved = [alloc("hh_moved_%d" % c, [P, PACK, CHUNK], BF16) for c in range(CHUNKS)]

        def make_hidden(g, c):
            nc.scalar.activation(out=share[g][c][:], in_=exponent[g][:, :, cols(c)], func=ACT.Sigmoid, scale=-1.0)
            for t in range(2):
                nc.vector.scalar_tensor_tensor(out=hh[g][c][:, t, :], in0=share[g][c][:, t, :],
                                               scalar=feature_cols[:, 0, g, t, 0:1], in1=z2_bank[g][t][:, cols(c)],
                                               op0=ALU.mult, op1=ALU.mult)
            nc.sync.dma_start(out=hh_moved[c][rows(g), :, :].rearrange("p (s t) n -> p s (t n)", s=2),
                              in_=hh[g][c][:].rearrange("q t n -> q (t n)"))

        hh_packed = alloc("hh_packed", [P, N * PACK], BF16)
        hh_codes = [alloc("hh_codes_%d" % g, [P, N], U32) for g in range(G)]
        hh_scales = [alloc("hh_scales_%d" % g, [P, N], U8) for g in range(G)]
        tanh_y = tiles_gt("tanh_y", [P, N], F32)
        result = tiles_gt("result", [P, N], F32)

        def pack_hidden(copy, g, c):
            interleave(copy, hh_packed, hh_moved[c][rows(g), :, :], rows(g), CHUNK * c, CHUNK * (c + 1))

        def quantize_hidden(g, c):
            quantize(hh_packed, hh_codes[g], hh_scales[g], slice(0, ROWS * (g + 1)), CHUNK * c, CHUNK * (c + 1))

        def finish(g, u, h):
            half = slice(HALF * h, HALF * (h + 1))
            nc.scalar.activation(out=tanh_y[g][u][:, half], in_=y_bank[g][u][:, half], func=ACT.Tanh,
                                 bias=ob_cols[:, g, u, 0:1])
            nc.vector.tensor_scalar(out=result[g][u][:, half], in0=tanh_y[g][u][:, half],
                                    scalar1=osc_cols[:, g, u, 0:1], scalar2=None, op0=ALU.mult)
            nc.sync.dma_start(out=out[g, P * u:P * (u + 1), half], in_=result[g][u][:, half])

        for row in (hs_row, fl_row, ob_row, osc_row):
            nc.vector.memset(row[:], 0.0)
        load_operand(x_raw, x)
        load_feature_vector(hs_row, hs)
        load_feature_vector(fl_row, fl)
        load_output_vector(ob_row, ob)
        load_output_vector(osc_row, osc)
        load_operand(w2_raw, w2)
        load_operand(w1_raw, w1)
        load_operand(wo_raw, wo2)

        interleave(on_scalar, xq[0], x_raw[:, :, X_SPLIT:N], everywhere, X_SPLIT, N)
        interleave(on_vector, xq[0], x_raw[:, :, 0:HALF], everywhere, 0, HALF)
        interleave(on_vector, xq[0], x_raw[:, :, HALF:X_SPLIT], everywhere, HALF, X_SPLIT)
        quantize(*xq, everywhere, 0, HALF)
        interleave_parity(on_scalar, w2q[0], w2_raw, 1)
        interleave_parity(on_vector, w2q[0], w2_raw, 0)
        quantize(*xq, everywhere, HALF, N)
        for t in range(2):
            first_layer(z2_bank, w2q, t)
        interleave_parity(on_scalar, w1q[0], w1_raw, 1)
        interleave_parity(on_vector, w1q[0], w1_raw, 0)
        split_feature_vectors_by_parity()
        for t in range(2):
            first_layer(z1_bank, w1q, t)

        square_on_scalar(0, 0)
        copy_out(z2_copy, z2_bank, 1, 0)
        turn_output_vectors()
        square_on_vector(sq2, z2_copy, z2_bank, 1, 0)
        second_bell(0, 0)
        square_on_scalar(0, 1)
        copy_out(z2_copy, z2_bank, 1, 1)
        turn_feature_vectors()
        square_on_vector(sq2, z2_copy, z2_bank, 1, 1)
        second_bell(1, 0)
        second_bell(0, 1)
        second_bell(1, 1)

        order = [(g, t) for g in range(G) for t in range(2)]
        for g, t in order:
            copy_out(z1_copy, z1_bank, g, t)
        for t in range(2):
            nc.gpsimd.tensor_tensor(out=sq1[0][t][:], in0=z1_copy[0][t][:], in1=z1_copy[0][t][:], op=ALU.mult)
            square_on_vector(sq1, z1_copy, z1_bank, 1, t)

        for g, t in order:
            make_exponent(g, t)

        interleave(on_vector, woq[0], wo_raw[:], everywhere, 0, O)

        for g in range(G):
            for c in range(CHUNKS):
                make_hidden(g, c)
        for g in range(G):
            for c in range(0, CHUNKS, 2):
                pack_hidden(on_vector, g, c)
                pack_hidden(on_scalar, g, c + 1)
                if (g, c) == (0, 0):
                    quantize(*woq, everywhere, 0, O)
            for c in range(CHUNKS):
                quantize_hidden(g, c)
            for u in range(2):
                matmul(y_bank[g][u], g, woq, u, hh_codes[g], hh_scales[g])
        for g in range(G):
            for u in range(2):
                for h in range(2):
                    finish(g, u, h)
